import numpy as np
import ml_dtypes


def mxq(x, axis, fmt="e4m3"):
    dtype, down = {"e4m3": (ml_dtypes.float8_e4m3fn, 7), "e5m2": (ml_dtypes.float8_e5m2, 14)}[fmt]
    v = np.moveaxis(np.asarray(x, np.float32).astype(ml_dtypes.bfloat16).astype(np.float64), axis, -1)
    blocks = v.reshape(v.shape[:-1] + (-1, 32))
    amax = np.abs(blocks).max(-1, keepdims=True)
    byte = np.maximum(np.where(amax > 0, np.frexp(amax)[1] - 1 + 127, 0) - down, 1)
    scale = np.exp2(byte - 127.0)
    codes = (blocks / scale).astype(np.float32).astype(dtype).astype(np.float64)
    return np.moveaxis((codes * scale).reshape(v.shape), -1, axis)


WIDE = False


def mx_kscale(k):
    if not WIDE:
        return np.ones(k)
    levels = np.array([10, -10, 5, -5, 0])
    if k % 512:
        return np.exp2(np.random.permutation(np.resize(levels, k // 32))).repeat(32)
    a = np.empty((k // 512, 16))
    for p in range(k // 512):
        a[p, :8] = np.random.permutation(np.resize(levels, 8))
        for g in range(8):
            far = levels[np.abs(levels - a[p, g]) >= 10]
            a[p, g + 8] = far[np.random.randint(len(far))]
    return np.exp2(a.ravel()).repeat(32)


def f64(x):
    return np.asarray(x).astype(np.float64)


def striped(idx):
    return np.tile(idx.reshape(-1, 16).T, (8, 1)).astype(np.uint16)


def unstriped(offs):
    return offs[:16].T.reshape(-1).astype(np.int64)


E2M1 = np.array([0.0, 0.5, 1.0, 1.5, 2.0, 3.0, 4.0, 6.0, -0.0, -0.5, -1.0, -1.5, -2.0, -3.0, -4.0, -6.0])


def pack_weight(w, fmt):
    k, n = w.shape
    w = f64(np.asarray(w, np.float32).astype(ml_dtypes.bfloat16)).reshape(k // 32, 32, n)
    amax = np.abs(w).max(1)
    if fmt == "e4m3":
        byte = np.frexp(amax)[1] - 1 + 127 - 7
    else:
        mant, ex = np.frexp(amax / 6.0)
        byte = np.where(mant > 0.5, ex, ex - 1) + 127
    byte = np.clip(np.where(amax > 0, byte, 1), 1, 254)
    scaled = (w * np.exp2(127.0 - byte)[:, None, :]).reshape(k, n).astype(np.float32)
    by_word = np.ascontiguousarray(scaled.reshape(k // 512, 128, 4, n).transpose(0, 1, 3, 2))
    if fmt == "e4m3":
        words = by_word.astype(ml_dtypes.float8_e4m3fn).view(np.uint8)
    else:
        c = by_word.astype(ml_dtypes.float4_e2m1fn).view(np.uint8) & 0xF
        words = (c[..., 0::2] | (c[..., 1::2] << 4)).reshape(k // 512, 128, 2 * n)
    return np.ascontiguousarray(words), np.ascontiguousarray(byte.astype(np.uint8).reshape(k // 512, 16, n))


def unpack_weight(words, scales, fmt):
    g, _, n = scales.shape
    words = np.ascontiguousarray(words).reshape(g, 128, n, -1)
    if fmt == "e4m3":
        vals = words.view(ml_dtypes.float8_e4m3fn).astype(np.float64)
    else:
        nib = np.empty((g, 128, n, 4), np.uint8)
        nib[..., 0::2] = words & 0xF
        nib[..., 1::2] = words >> 4
        vals = E2M1[nib]
    vals = vals * np.repeat(np.exp2(scales.astype(np.float64) - 127.0), 8, axis=1)[..., None]
    return vals.transpose(0, 1, 3, 2).reshape(g * 512, n)


K, T, E, C, N = 384, 640, 20, 128, 512
TOP = 4


def by_expert(wq, xq):
    return np.concatenate([wq[e].T @ xq[:, e * C:(e + 1) * C] for e in range(E)], axis=1)


def setup_inputs():
    n = np.random.standard_normal
    s = mx_kscale(N)[:, None]
    deal = np.repeat(np.arange(E), C).reshape(TOP, T)[:, np.random.permutation(T)]
    deal = np.take_along_axis(deal, np.argsort(np.random.rand(TOP, T), axis=0), axis=0)
    for _ in range(8):
        s_, t_ = np.random.permutation(T).reshape(2, -1); r = np.random.randint(TOP, size=T // 2); x, y = deal[r, s_].copy(), deal[r, t_].copy()
        ok = ~((deal[:, s_] == y).any(0) | (deal[:, t_] == x).any(0)); deal[r[ok], s_[ok]] = y[ok]; deal[r[ok], t_[ok]] = x[ok]
    order = np.lexsort((np.random.rand(TOP * T), deal.reshape(-1)))
    slot_token = order % T; pos = np.empty(TOP * T, np.int64); pos[order] = np.arange(TOP * T); pos = pos.reshape(TOP, T)
    g = np.random.uniform(0.5, 1.5, (TOP, T)); g = g / g.sum(0)
    w_slot = np.empty(E * C)
    for r in range(TOP): w_slot[pos[r]] = g[r]
    w = [pack_weight(m, "e2m1") for m in n((E, N, K)) / np.sqrt(N) / s[None]]
    return {
        "dyT": (n((N, T)) * s).astype(np.float32),
        "w_words": np.stack([m[0] for m in w]),
        "w_scales": np.stack([m[1] for m in w]),
        "gate": np.tile(w_slot, (N, 1)).astype(np.float32),
        "offs": striped(slot_token),
        "pos1": striped(pos[0]),
        "pos2": striped(pos[1]),
        "pos3": striped(pos[2]),
        "pos4": striped(pos[3]),
    }


def reference(dyT, w_words, w_scales, gate, offs, pos1, pos2, pos3, pos4):
    idx = unstriped(offs)
    w = np.stack([unpack_weight(w_words[e], w_scales[e], "e2m1") for e in range(E)])
    gq = mxq(f64(gate) * f64(dyT)[:, idx], 0, "e4m3")
    dx = by_expert(w, gq)
    return dx[:, unstriped(pos1)] + dx[:, unstriped(pos2)] + dx[:, unstriped(pos3)] + dx[:, unstriped(pos4)]

@@ -1,0 +1,207 @@
+from contextlib import ExitStack
+
+import concourse.mybir as mybir
+from concourse.masks import make_identity
+
+K, T, E, C, N = 384, 640, 20, 128, 512
+TOP = 4
+S = E * C
+
+FLOPS = 2 * K * N * S
+BYTES = 4 * N * T + E * 128 * 768 + E * 16 * K + 4 * S + 2 * 128 * (S // 16) * 2 + 4 * K * T
+
+F32 = mybir.dt.float32
+BF16 = mybir.dt.bfloat16
+I32 = mybir.dt.int32
+U32 = mybir.dt.uint32
+U16 = mybir.dt.uint16
+U8 = mybir.dt.uint8
+FP8X4 = mybir.dt.float8_e4m3fn_x4
+FP4X4 = mybir.dt.float4_e2m1fn_x4
+MULT = mybir.AluOpType.mult
+ADD = mybir.AluOpType.add
+
+P = 128
+PACK = 4
+KT = K // P
+BANK = 512
+CHUNKS = (256, 512, 512, 512, 256, 256, 128, 128)
+GATE_LOADS = (256, 512, 1024, 768)
+W_LOADS = (6, 7, 7)
+TOKEN_GROUPS = ((0, 384), (384, 640))
+HALF = T // 2
+
+
+def starts(widths):
+    return [sum(widths[:i]) for i in range(len(widths))]
+
+
+def tile_moe_bdx_lin_none_kernel(tc, dyT, w_words, w_scales, gate, offs, pos1, pos2, pos3, pos4, out):
+    nc = tc.nc
+    with ExitStack() as ctx:
+        lists = ctx.enter_context(tc.tile_pool(name="lists", bufs=1))
+        keep = ctx.enter_context(tc.tile_pool(name="keep", bufs=1))
+        acc_pool = ctx.enter_context(tc.psum_pool(name="acc", bufs=4))
+        turn_pool = ctx.enter_context(tc.psum_pool(name="turn", bufs=2))
+
+        offs_sb = lists.tile([P, S // 16], U16, name="offs_sb")
+        pos_sb = [lists.tile([P, T // 16], U16, name="pos_sb%d" % r) for r in range(TOP)]
+        dy = [keep.tile([P, T], F32, name="dy%d" % t) for t in range(PACK)]
+        gate_sb = keep.tile([P, S], F32, name="gate_sb")
+        w_sb = keep.tile([P, E, 2 * K], U8, name="w_sb", align_bytes=64)
+        ws_sb = keep.tile([P, E, K], U8, name="ws_sb", align_bytes=64)
+        g_codes = keep.tile([P, S], U32, name="g_codes", align_bytes=64)
+        g_scales = keep.tile([P, S], U8, name="g_scales", align_bytes=64)
+        dx = [keep.tile([P, S], F32, name="dx%d" % j) for j in range(KT)]
+        ident = keep.tile([P, P], F32, name="ident")
+
+        nc.vector.memset(ws_sb[:].bitcast(I32), 0)
+        make_identity(nc, ident[:])
+
+        dy_rows = dyT.rearrange("(p t) j -> p t j", t=PACK)
+        gate_at = starts(GATE_LOADS)
+
+        def load_gate(i):
+            cols = slice(gate_at[i], gate_at[i] + GATE_LOADS[i])
+            nc.sync.dma_start(gate_sb[:, cols], gate[0:P, cols])
+
+        nc.sync.dma_start(offs_sb[:], offs)
+        nc.sync.dma_start(dy[0][:], dy_rows[:, 0, :])
+        load_gate(0)
+        for t in range(1, PACK):
+            nc.sync.dma_start(dy[t][:], dy_rows[:, t, :])
+        for i in range(1, len(GATE_LOADS)):
+            load_gate(i)
+        for e0, ne in zip(starts(W_LOADS), W_LOADS):
+            nc.sync.dma_start(
+                w_sb[:, e0 : e0 + ne, :].bitcast(I32),
+                w_words[e0 : e0 + ne, 0].rearrange("e p b -> p e b").bitcast(I32),
+            )
+        for q in range(4):
+            nc.sync.dma_start(
+                ws_sb[32 * q : 32 * q + 4].bitcast(I32),
+                w_scales[:, 0, 4 * q : 4 * q + 4, :].rearrange("e r k -> r e k").bitcast(I32),
+            )
+        for r, pos in enumerate((pos1, pos2, pos3, pos4)):
+            nc.sync.dma_start(pos_sb[r][:], pos)
+
+        chunk_at = starts(CHUNKS)
+        planes = {}
+        grouped = {}
+
+        def gather(c):
+            s0, n = chunk_at[c], CHUNKS[c]
+            planes[c] = keep.tile([P, PACK, n], F32, name="planes%d" % c)
+            for t in range(PACK):
+                nc.vector.tensor_tensor(
+                    planes[c][:, t, :],
+                    dy[t][:].indirect(offs_sb[:, s0 // 16 : (s0 + n) // 16]),
+                    gate_sb[:, s0 : s0 + n],
+                    MULT,
+                )
+
+        def interleave(c):
+            n = CHUNKS[c]
+            grouped[c] = keep.tile([P, n, PACK], BF16, name="grouped%d" % c, align_bytes=64)
+            nc.scalar.copy(
+                grouped[c][:].rearrange("p (a i) t -> p a t i", i=4),
+                planes[c][:].rearrange("p t (a i) -> p a t i", i=4),
+            )
+
+        def quantize(c):
+            s0, n = chunk_at[c], CHUNKS[c]
+            nc.vector.quantize_mx(
+                out=g_codes[:, s0 : s0 + n].bitcast(FP8X4),
+                scales=g_scales[:, s0 : s0 + n],
+                in_=grouped[c][:].rearrange("p s t -> p (s t)"),
+            )
+
+        def multiply(j, s0, n):
+            acc = acc_pool.tile([P, BANK], F32, name="acc")
+            for s in range(s0, s0 + n, C):
+                e = s // C
+                nc.tensor.matmul_mx(
+                    out=acc[:, s - s0 : s - s0 + C],
+                    lhsT=w_sb[:, e, 2 * P * j : 2 * P * (j + 1)].bitcast(FP4X4),
+                    lhsT_scale=ws_sb[:, e, P * j : P * (j + 1)],
+                    rhs=g_codes[:, s : s + C].bitcast(FP8X4),
+                    rhs_scale=g_scales[:, s : s + C],
+                    start=True,
+                    stop=True,
+                )
+            nc.scalar.copy(dx[j][:, s0 : s0 + n], acc[:, 0:n])
+
+        LAG = 2
+        for c in range(len(CHUNKS) + LAG):
+            if c < len(CHUNKS):
+                gather(c)
+                interleave(c)
+            if c >= LAG:
+                quantize(c - LAG)
+                multiply(0, chunk_at[c - LAG], CHUNKS[c - LAG])
+        for j in range(1, KT):
+            for s0 in range(0, S, BANK):
+                multiply(j, s0, BANK)
+
+        picked = {}
+
+        def fetch(j, r, t0=0, t1=T):
+            if (j, r) not in picked:
+                picked[j, r] = keep.tile([P, T], F32, name="picked%d_%d" % (j, r))
+            nc.vector.tensor_copy(picked[j, r][:, t0:t1], dx[j][:].indirect(pos_sb[r][:, t0 // 16 : t1 // 16]))
+
+        def add_on_tensor(j, terms):
+            turned = keep.tile([P, T], F32, name="turned%d" % j)
+            sums = []
+            for g, (t0, t1) in enumerate(TOKEN_GROUPS):
+                bank = turn_pool.tile([P, BANK], F32, name="turn%d" % g)
+                for t in range(t0, t1, P):
+                    for r in range(terms):
+                        nc.tensor.matmul(
+                            bank[:, t - t0 : t - t0 + P],
+                            picked[j, r][:, t : t + P],
+                            ident[:],
+                            start=(r == 0),
+                            stop=(r == terms - 1),
+                            is_transpose=True,
+                        )
+                nc.scalar.copy(turned[:, t0:t1], bank[:, 0 : t1 - t0])
+            for g, (t0, t1) in enumerate(TOKEN_GROUPS):
+                back = acc_pool.tile([P, BANK], F32, name="acc")
+                for t in range(t0, t1, P):
+                    nc.tensor.transpose(back[:, t - t0 : t - t0 + P], turned[:, t : t + P], ident[:])
+                sums.append(back)
+            return sums
+
+        result = [keep.tile([P, T], F32, name="result%d" % j) for j in range(KT)]
+
+        def store(j, t0, t1):
+            nc.sync.dma_start(out[P * j : P * (j + 1), t0:t1], result[j][:, t0:t1])
+
+        def add_last(j, sums, t0, t1):
+            for g, (g0, g1) in enumerate(TOKEN_GROUPS):
+                a, b = max(t0, g0), min(t1, g1)
+                if a < b:
+                    nc.vector.tensor_tensor(
+                        result[j][:, a:b], sums[g][:, a - g0 : b - g0], picked[j, TOP - 1][:, a:b], ADD
+                    )
+            store(j, t0, t1)
+
+        for r in range(TOP):
+            fetch(0, r)
+        sums0 = add_on_tensor(0, TOP)
+        for g, (t0, t1) in enumerate(TOKEN_GROUPS):
+            nc.scalar.copy(result[0][:, t0:t1], sums0[g][:, 0 : t1 - t0])
+        store(0, 0, T)
+
+        sums = {}
+        for j in (1, 2):
+            for r in range(TOP - 1):
+                fetch(j, r)
+            sums[j] = add_on_tensor(j, TOP - 1)
+        fetch(1, TOP - 1)
+        fetch(2, TOP - 1, HALF, T)
+        add_last(1, sums[1], 0, T)
+        fetch(2, TOP - 1, 0, HALF)
+        add_last(2, sums[2], HALF, T)
+        add_last(2, sums[2], 0, HALF)

@@ -25,10 +25,11 @@ P = 128
 PACK = 4
 KT = K // P
 BANK = 512
-CHUNKS = (256, 512, 512, 512, 256, 256, 128, 128)
-GATE_LOADS = (256, 512, 1024, 768)
+CHUNKS = (384, 1024, 512, 384, 256)
+WINDOW = max(T, max(CHUNKS) + 16)
+GATE_LOADS = (384, 1024, 1152)
 W_LOADS = (6, 7, 7)
-TOKEN_GROUPS = ((0, 384), (384, 640))
+TOKEN_GROUPS = ((384, 640), (0, 384))
 HALF = T // 2
 
 
@@ -36,42 +37,54 @@ def starts(widths):
     return [sum(widths[:i]) for i in range(len(widths))]
 
 
+def pieces(s0, n):
+    cut = []
+    for width in (512, 256, 128):
+        while n >= width:
+            cut.append((s0, width))
+            s0, n = s0 + width, n - width
+    return cut
+
+
 def tile_moe_bdx_lin_none_kernel(tc, dyT, w_words, w_scales, gate, offs, pos1, pos2, pos3, pos4, out):
     nc = tc.nc
     with ExitStack() as ctx:
         lists = ctx.enter_context(tc.tile_pool(name="lists", bufs=1))
         keep = ctx.enter_context(tc.tile_pool(name="keep", bufs=1))
-        acc_pool = ctx.enter_context(tc.psum_pool(name="acc", bufs=4))
-        turn_pool = ctx.enter_context(tc.psum_pool(name="turn", bufs=2))
+        psum = ctx.enter_context(tc.psum_pool(name="psum", bufs=8))
 
         offs_sb = lists.tile([P, S // 16], U16, name="offs_sb")
         pos_sb = [lists.tile([P, T // 16], U16, name="pos_sb%d" % r) for r in range(TOP)]
-        dy = [keep.tile([P, T], F32, name="dy%d" % t) for t in range(PACK)]
+        dy = [keep.tile([P, WINDOW], F32, name="dy%d" % t) for t in range(PACK)]
         gate_sb = keep.tile([P, S], F32, name="gate_sb")
         w_sb = keep.tile([P, E, 2 * K], U8, name="w_sb", align_bytes=64)
         ws_sb = keep.tile([P, E, K], U8, name="ws_sb", align_bytes=64)
+        grouped = keep.tile([P, S, PACK], BF16, name="grouped", align_bytes=64)
         g_codes = keep.tile([P, S], U32, name="g_codes", align_bytes=64)
         g_scales = keep.tile([P, S], U8, name="g_scales", align_bytes=64)
         dx = [keep.tile([P, S], F32, name="dx%d" % j) for j in range(KT)]
         ident = keep.tile([P, P], F32, name="ident")
 
-        nc.vector.memset(ws_sb[:].bitcast(I32), 0)
+        if WINDOW > T:
+            for t in range(PACK):
+                nc.gpsimd.memset(dy[t][:, T:], 0.0)
         make_identity(nc, ident[:])
+        nc.gpsimd.memset(ws_sb[:].bitcast(I32), 0)
 
         dy_rows = dyT.rearrange("(p t) j -> p t j", t=PACK)
         gate_at = starts(GATE_LOADS)
 
-        def load_gate(i):
+        def load_gate(i, queue):
             cols = slice(gate_at[i], gate_at[i] + GATE_LOADS[i])
-            nc.sync.dma_start(gate_sb[:, cols], gate[0:P, cols])
+            queue.dma_start(gate_sb[:, cols], gate[0:P, cols])
 
         nc.sync.dma_start(offs_sb[:], offs)
-        nc.sync.dma_start(dy[0][:], dy_rows[:, 0, :])
-        load_gate(0)
+        nc.sync.dma_start(dy[0][:, 0:T], dy_rows[:, 0, :])
+        load_gate(0, nc.scalar)
         for t in range(1, PACK):
-            nc.sync.dma_start(dy[t][:], dy_rows[:, t, :])
+            nc.sync.dma_start(dy[t][:, 0:T], dy_rows[:, t, :])
         for i in range(1, len(GATE_LOADS)):
-            load_gate(i)
+            load_gate(i, nc.sync)
         for e0, ne in zip(starts(W_LOADS), W_LOADS):
             nc.sync.dma_start(
                 w_sb[:, e0 : e0 + ne, :].bitcast(I32),
@@ -86,38 +99,34 @@ def tile_moe_bdx_lin_none_kernel(tc, dyT, w_words, w_scales, gate, offs, pos1, p
             nc.sync.dma_start(pos_sb[r][:], pos)
 
         chunk_at = starts(CHUNKS)
-        planes = {}
-        grouped = {}
 
         def gather(c):
             s0, n = chunk_at[c], CHUNKS[c]
-            planes[c] = keep.tile([P, PACK, n], F32, name="planes%d" % c)
+            planes = keep.tile([P, PACK, n], F32, name="planes%d" % c)
             for t in range(PACK):
                 nc.vector.tensor_tensor(
-                    planes[c][:, t, :],
+                    planes[:, t, :],
                     dy[t][:].indirect(offs_sb[:, s0 // 16 : (s0 + n) // 16]),
                     gate_sb[:, s0 : s0 + n],
                     MULT,
                 )
+            return planes
 
-        def interleave(c):
-            n = CHUNKS[c]
-            grouped[c] = keep.tile([P, n, PACK], BF16, name="grouped%d" % c, align_bytes=64)
-            nc.scalar.copy(
-                grouped[c][:].rearrange("p (a i) t -> p a t i", i=4),
-                planes[c][:].rearrange("p t (a i) -> p a t i", i=4),
+        def interleave(copy, planes, s0, s, m):
+            copy(
+                grouped[:, s : s + m, :].rearrange("p (a i) t -> p a t i", i=4),
+                planes[:, :, s - s0 : s - s0 + m].rearrange("p t (a i) -> p a t i", i=4),
             )
 
-        def quantize(c):
-            s0, n = chunk_at[c], CHUNKS[c]
+        def quantize(s0, n):
             nc.vector.quantize_mx(
                 out=g_codes[:, s0 : s0 + n].bitcast(FP8X4),
                 scales=g_scales[:, s0 : s0 + n],
-                in_=grouped[c][:].rearrange("p s t -> p (s t)"),
+                in_=grouped[:, s0 : s0 + n, :].rearrange("p s t -> p (s t)"),
             )
 
-        def multiply(j, s0, n):
-            acc = acc_pool.tile([P, BANK], F32, name="acc")
+        def multiply(j, s0, n, on_vector=False):
+            acc = psum.tile([P, BANK], F32, name="bank")
             for s in range(s0, s0 + n, C):
                 e = s // C
                 nc.tensor.matmul_mx(
@@ -129,16 +138,27 @@ def tile_moe_bdx_lin_none_kernel(tc, dyT, w_words, w_scales, gate, offs, pos1, p
                     start=True,
                     stop=True,
                 )
-            nc.scalar.copy(dx[j][:, s0 : s0 + n], acc[:, 0:n])
+            if on_vector:
+                nc.vector.tensor_copy(dx[j][:, s0 : s0 + n], acc[:, 0:n])
+            else:
+                nc.scalar.copy(dx[j][:, s0 : s0 + n], acc[:, 0:n])
 
-        LAG = 2
-        for c in range(len(CHUNKS) + LAG):
-            if c < len(CHUNKS):
-                gather(c)
-                interleave(c)
-            if c >= LAG:
-                quantize(c - LAG)
-                multiply(0, chunk_at[c - LAG], CHUNKS[c - LAG])
+        last = len(CHUNKS) - 1
+        for c in range(len(CHUNKS)):
+            s0, n = chunk_at[c], CHUNKS[c]
+            planes = gather(c)
+            on_scalar = n if c < last else n - C
+            for s, m in pieces(s0, on_scalar):
+                interleave(nc.scalar.copy, planes, s0, s, m)
+            if c > 0:
+                for s, m in pieces(chunk_at[c - 1], CHUNKS[c - 1]):
+                    quantize(s, m)
+                for s, m in pieces(chunk_at[c - 1], CHUNKS[c - 1]):
+                    multiply(0, s, m)
+        interleave(nc.vector.tensor_copy, planes, s0, S - C, C)
+        quantize(s0, n)
+        multiply(0, s0, n - C)
+        multiply(0, S - C, C, on_vector=True)
         for j in range(1, KT):
             for s0 in range(0, S, BANK):
                 multiply(j, s0, BANK)
@@ -150,24 +170,15 @@ def tile_moe_bdx_lin_none_kernel(tc, dyT, w_words, w_scales, gate, offs, pos1, p
                 picked[j, r] = keep.tile([P, T], F32, name="picked%d_%d" % (j, r))
             nc.vector.tensor_copy(picked[j, r][:, t0:t1], dx[j][:].indirect(pos_sb[r][:, t0 // 16 : t1 // 16]))
 
-        def add_on_tensor(j, terms):
-            turned = keep.tile([P, T], F32, name="turned%d" % j)
+        def turn_add(dst, j, r, t, terms):
+            nc.tensor.matmul(
+                dst, picked[j, r][:, t : t + P], ident[:], start=(r == 0), stop=(r == terms - 1), is_transpose=True
+            )
+
+        def turn_back(turned):
             sums = []
-            for g, (t0, t1) in enumerate(TOKEN_GROUPS):
-                bank = turn_pool.tile([P, BANK], F32, name="turn%d" % g)
-                for t in range(t0, t1, P):
-                    for r in range(terms):
-                        nc.tensor.matmul(
-                            bank[:, t - t0 : t - t0 + P],
-                            picked[j, r][:, t : t + P],
-                            ident[:],
-                            start=(r == 0),
-                            stop=(r == terms - 1),
-                            is_transpose=True,
-                        )
-                nc.scalar.copy(turned[:, t0:t1], bank[:, 0 : t1 - t0])
-            for g, (t0, t1) in enumerate(TOKEN_GROUPS):
-                back = acc_pool.tile([P, BANK], F32, name="acc")
+            for t0, t1 in TOKEN_GROUPS:
+                back = psum.tile([P, BANK], F32, name="bank")
                 for t in range(t0, t1, P):
                     nc.tensor.transpose(back[:, t - t0 : t - t0 + P], turned[:, t : t + P], ident[:])
                 sums.append(back)
@@ -178,30 +189,35 @@ def tile_moe_bdx_lin_none_kernel(tc, dyT, w_words, w_scales, gate, offs, pos1, p
         def store(j, t0, t1):
             nc.sync.dma_start(out[P * j : P * (j + 1), t0:t1], result[j][:, t0:t1])
 
-        def add_last(j, sums, t0, t1):
-            for g, (g0, g1) in enumerate(TOKEN_GROUPS):
-                a, b = max(t0, g0), min(t1, g1)
-                if a < b:
-                    nc.vector.tensor_tensor(
-                        result[j][:, a:b], sums[g][:, a - g0 : b - g0], picked[j, TOP - 1][:, a:b], ADD
-                    )
-            store(j, t0, t1)
-
-        for r in range(TOP):
-            fetch(0, r)
-        sums0 = add_on_tensor(0, TOP)
-        for g, (t0, t1) in enumerate(TOKEN_GROUPS):
-            nc.scalar.copy(result[0][:, t0:t1], sums0[g][:, 0 : t1 - t0])
-        store(0, 0, T)
-
-        sums = {}
-        for j in (1, 2):
-            for r in range(TOP - 1):
+        for j in range(KT - 1):
+            for r in range(TOP):
                 fetch(j, r)
-            sums[j] = add_on_tensor(j, TOP - 1)
-        fetch(1, TOP - 1)
-        fetch(2, TOP - 1, HALF, T)
-        add_last(1, sums[1], 0, T)
-        fetch(2, TOP - 1, 0, HALF)
-        add_last(2, sums[2], HALF, T)
-        add_last(2, sums[2], 0, HALF)
+            turned = keep.tile([P, T], F32, name="turned%d" % j)
+            for t0, t1 in TOKEN_GROUPS:
+                bank = psum.tile([P, BANK], F32, name="bank")
+                for t in range(t0, t1, P):
+                    for r in range(TOP):
+                        turn_add(bank[:, t - t0 : t - t0 + P], j, r, t, TOP)
+                nc.scalar.copy(turned[:, t0:t1], bank[:, 0 : t1 - t0])
+            for (t0, t1), back in zip(TOKEN_GROUPS, turn_back(turned)):
+                nc.scalar.copy(result[j][:, t0:t1], back[:, 0 : t1 - t0])
+            store(j, 0, T)
+
+        j = KT - 1
+        blocks = [t for t0, t1 in TOKEN_GROUPS for t in range(t0, t1, P)]
+        turned = keep.tile([P, T], F32, name="turned%d" % j)
+        banks = {}
+        for r in range(TOP - 1):
+            fetch(j, r)
+            for t in blocks:
+                if r == 0:
+                    banks[t] = psum.tile([P, BANK], F32, name="bank")
+                turn_add(banks[t][:, 0:P], j, r, t, TOP - 1)
+        for t in blocks:
+            nc.scalar.copy(turned[:, t : t + P], banks[t][:, 0:P])
+        sums = turn_back(turned)
+        fetch(j, TOP - 1, HALF, T)
+        fetch(j, TOP - 1, 0, HALF)
+        for (t0, t1), back in zip(TOKEN_GROUPS, sums):
+            nc.vector.tensor_tensor(result[j][:, t0:t1], back[:, 0 : t1 - t0], picked[j, TOP - 1][:, t0:t1], ADD)
+            store(j, t0, t1)

@@ -25,11 +25,12 @@ P = 128
 PACK = 4
 KT = K // P
 BANK = 512
-CHUNKS = (384, 1024, 512, 384, 256)
+CHUNKS = (384, 896, 640, 384, 256)
 WINDOW = max(T, max(CHUNKS) + 16)
-GATE_LOADS = (384, 1024, 1152)
+GATE_LOADS = (384, 896, 1280)
 W_LOADS = (6, 7, 7)
 TOKEN_GROUPS = ((384, 640), (0, 384))
+LAST_GROUPS = ((0, 256), (256, 512), (512, 640))
 HALF = T // 2
 
 
@@ -46,12 +47,19 @@ def pieces(s0, n):
     return cut
 
 
+def halves(s0, n):
+    if n <= BANK:
+        return [(s0, n)]
+    first = (n // C + 1) // 2 * C
+    return [(s0, first), (s0 + first, n - first)]
+
+
 def tile_moe_bdx_lin_none_kernel(tc, dyT, w_words, w_scales, gate, offs, pos1, pos2, pos3, pos4, out):
     nc = tc.nc
     with ExitStack() as ctx:
         lists = ctx.enter_context(tc.tile_pool(name="lists", bufs=1))
         keep = ctx.enter_context(tc.tile_pool(name="keep", bufs=1))
-        psum = ctx.enter_context(tc.psum_pool(name="psum", bufs=8))
+        psum = ctx.enter_context(tc.psum_pool(name="psum", bufs=1))
 
         offs_sb = lists.tile([P, S // 16], U16, name="offs_sb")
         pos_sb = [lists.tile([P, T // 16], U16, name="pos_sb%d" % r) for r in range(TOP)]
@@ -65,11 +73,14 @@ def tile_moe_bdx_lin_none_kernel(tc, dyT, w_words, w_scales, gate, offs, pos1, p
         dx = [keep.tile([P, S], F32, name="dx%d" % j) for j in range(KT)]
         ident = keep.tile([P, P], F32, name="ident")
 
+        def bank(b):
+            return psum.tile([P, BANK], F32, name="bank%d" % b)
+
         if WINDOW > T:
             for t in range(PACK):
-                nc.gpsimd.memset(dy[t][:, T:], 0.0)
+                nc.vector.memset(dy[t][:, T:], 0.0)
         make_identity(nc, ident[:])
-        nc.gpsimd.memset(ws_sb[:].bitcast(I32), 0)
+        nc.vector.memset(ws_sb[:].bitcast(I32), 0)
 
         dy_rows = dyT.rearrange("(p t) j -> p t j", t=PACK)
         gate_at = starts(GATE_LOADS)
@@ -125,8 +136,8 @@ def tile_moe_bdx_lin_none_kernel(tc, dyT, w_words, w_scales, gate, offs, pos1, p
                 in_=grouped[:, s0 : s0 + n, :].rearrange("p s t -> p (s t)"),
             )
 
-        def multiply(j, s0, n, on_vector=False):
-            acc = psum.tile([P, BANK], F32, name="bank")
+        def multiply(j, s0, n, b, on_vector=False):
+            acc = bank(b)
             for s in range(s0, s0 + n, C):
                 e = s // C
                 nc.tensor.matmul_mx(
@@ -144,24 +155,27 @@ def tile_moe_bdx_lin_none_kernel(tc, dyT, w_words, w_scales, gate, offs, pos1, p
                 nc.scalar.copy(dx[j][:, s0 : s0 + n], acc[:, 0:n])
 
         last = len(CHUNKS) - 1
+        used = 0
         for c in range(len(CHUNKS)):
             s0, n = chunk_at[c], CHUNKS[c]
             planes = gather(c)
             on_scalar = n if c < last else n - C
-            for s, m in pieces(s0, on_scalar):
+            for s, m in halves(s0, on_scalar):
                 interleave(nc.scalar.copy, planes, s0, s, m)
             if c > 0:
                 for s, m in pieces(chunk_at[c - 1], CHUNKS[c - 1]):
                     quantize(s, m)
-                for s, m in pieces(chunk_at[c - 1], CHUNKS[c - 1]):
-                    multiply(0, s, m)
+                for s, m in halves(chunk_at[c - 1], CHUNKS[c - 1]):
+                    multiply(0, s, m, used)
+                    used += 1
         interleave(nc.vector.tensor_copy, planes, s0, S - C, C)
         quantize(s0, n)
-        multiply(0, s0, n - C)
-        multiply(0, S - C, C, on_vector=True)
+        multiply(0, s0, n - C, 6)
+        multiply(0, S - C, C, 7, on_vector=True)
         for j in range(1, KT):
             for s0 in range(0, S, BANK):
-                multiply(j, s0, BANK)
+                multiply(j, s0, BANK, 5 + used % 3)
+                used += 1
 
         picked = {}
 
@@ -175,10 +189,10 @@ def tile_moe_bdx_lin_none_kernel(tc, dyT, w_words, w_scales, gate, offs, pos1, p
                 dst, picked[j, r][:, t : t + P], ident[:], start=(r == 0), stop=(r == terms - 1), is_transpose=True
             )
 
-        def turn_back(turned):
+        def turn_back(turned, groups, first_bank):
             sums = []
-            for t0, t1 in TOKEN_GROUPS:
-                back = psum.tile([P, BANK], F32, name="bank")
+            for g, (t0, t1) in enumerate(groups):
+                back = bank(first_bank + g)
                 for t in range(t0, t1, P):
                     nc.tensor.transpose(back[:, t - t0 : t - t0 + P], turned[:, t : t + P], ident[:])
                 sums.append(back)
@@ -193,31 +207,33 @@ def tile_moe_bdx_lin_none_kernel(tc, dyT, w_words, w_scales, gate, offs, pos1, p
             for r in range(TOP):
                 fetch(j, r)
             turned = keep.tile([P, T], F32, name="turned%d" % j)
-            for t0, t1 in TOKEN_GROUPS:
-                bank = psum.tile([P, BANK], F32, name="bank")
+            for g, (t0, t1) in enumerate(TOKEN_GROUPS):
+                acc = bank(g)
                 for t in range(t0, t1, P):
                     for r in range(TOP):
-                        turn_add(bank[:, t - t0 : t - t0 + P], j, r, t, TOP)
-                nc.scalar.copy(turned[:, t0:t1], bank[:, 0 : t1 - t0])
-            for (t0, t1), back in zip(TOKEN_GROUPS, turn_back(turned)):
+                        turn_add(acc[:, t - t0 : t - t0 + P], j, r, t, TOP)
+                nc.scalar.copy(turned[:, t0:t1], acc[:, 0 : t1 - t0])
+            for (t0, t1), back in zip(TOKEN_GROUPS, turn_back(turned, TOKEN_GROUPS, 2)):
                 nc.scalar.copy(result[j][:, t0:t1], back[:, 0 : t1 - t0])
             store(j, 0, T)
 
         j = KT - 1
-        blocks = [t for t0, t1 in TOKEN_GROUPS for t in range(t0, t1, P)]
+        blocks = list(range(0, T, P))
         turned = keep.tile([P, T], F32, name="turned%d" % j)
-        banks = {}
+        open_sums = {t: bank(b) for t, b in zip(blocks, (4, 5, 6, 7, 0))}
         for r in range(TOP - 1):
-            fetch(j, r)
+            if r < TOP - 2:
+                fetch(j, r)
+            else:
+                fetch(j, r, 0, HALF)
+                fetch(j, r, HALF, T)
             for t in blocks:
-                if r == 0:
-                    banks[t] = psum.tile([P, BANK], F32, name="bank")
-                turn_add(banks[t][:, 0:P], j, r, t, TOP - 1)
+                turn_add(open_sums[t][:, 0:P], j, r, t, TOP - 1)
         for t in blocks:
-            nc.scalar.copy(turned[:, t : t + P], banks[t][:, 0:P])
-        sums = turn_back(turned)
-        fetch(j, TOP - 1, HALF, T)
+            nc.scalar.copy(turned[:, t : t + P], open_sums[t][:, 0:P])
+        sums = turn_back(turned, LAST_GROUPS, 1)
         fetch(j, TOP - 1, 0, HALF)
-        for (t0, t1), back in zip(TOKEN_GROUPS, sums):
+        fetch(j, TOP - 1, HALF, T)
+        for (t0, t1), back in zip(LAST_GROUPS, sums):
             nc.vector.tensor_tensor(result[j][:, t0:t1], back[:, 0 : t1 - t0], picked[j, TOP - 1][:, t0:t1], ADD)
             store(j, t0, t1)

@@ -30,7 +30,6 @@ WINDOW = max(T, max(CHUNKS) + 16)
 GATE_LOADS = (384, 896, 1280)
 W_LOADS = (6, 7, 7)
 TOKEN_GROUPS = ((384, 640), (0, 384))
-LAST_GROUPS = ((0, 256), (256, 512), (512, 640))
 HALF = T // 2
 
 
@@ -59,7 +58,7 @@ def tile_moe_bdx_lin_none_kernel(tc, dyT, w_words, w_scales, gate, offs, pos1, p
     with ExitStack() as ctx:
         lists = ctx.enter_context(tc.tile_pool(name="lists", bufs=1))
         keep = ctx.enter_context(tc.tile_pool(name="keep", bufs=1))
-        psum = ctx.enter_context(tc.psum_pool(name="psum", bufs=1))
+        psum = ctx.enter_context(tc.psum_pool(name="psum", bufs=8))
 
         offs_sb = lists.tile([P, S // 16], U16, name="offs_sb")
         pos_sb = [lists.tile([P, T // 16], U16, name="pos_sb%d" % r) for r in range(TOP)]
@@ -73,12 +72,9 @@ def tile_moe_bdx_lin_none_kernel(tc, dyT, w_words, w_scales, gate, offs, pos1, p
         dx = [keep.tile([P, S], F32, name="dx%d" % j) for j in range(KT)]
         ident = keep.tile([P, P], F32, name="ident")
 
-        def bank(b):
-            return psum.tile([P, BANK], F32, name="bank%d" % b)
-
         if WINDOW > T:
             for t in range(PACK):
-                nc.vector.memset(dy[t][:, T:], 0.0)
+                nc.gpsimd.memset(dy[t][:, T:], 0.0)
         make_identity(nc, ident[:])
         nc.vector.memset(ws_sb[:].bitcast(I32), 0)
 
@@ -136,8 +132,8 @@ def tile_moe_bdx_lin_none_kernel(tc, dyT, w_words, w_scales, gate, offs, pos1, p
                 in_=grouped[:, s0 : s0 + n, :].rearrange("p s t -> p (s t)"),
             )
 
-        def multiply(j, s0, n, b, on_vector=False):
-            acc = bank(b)
+        def multiply(j, s0, n, on_vector=False):
+            acc = psum.tile([P, BANK], F32, name="bank")
             for s in range(s0, s0 + n, C):
                 e = s // C
                 nc.tensor.matmul_mx(
@@ -155,7 +151,6 @@ def tile_moe_bdx_lin_none_kernel(tc, dyT, w_words, w_scales, gate, offs, pos1, p
                 nc.scalar.copy(dx[j][:, s0 : s0 + n], acc[:, 0:n])
 
         last = len(CHUNKS) - 1
-        used = 0
         for c in range(len(CHUNKS)):
             s0, n = chunk_at[c], CHUNKS[c]
             planes = gather(c)
@@ -166,16 +161,14 @@ def tile_moe_bdx_lin_none_kernel(tc, dyT, w_words, w_scales, gate, offs, pos1, p
                 for s, m in pieces(chunk_at[c - 1], CHUNKS[c - 1]):
                     quantize(s, m)
                 for s, m in halves(chunk_at[c - 1], CHUNKS[c - 1]):
-                    multiply(0, s, m, used)
-                    used += 1
+                    multiply(0, s, m)
         interleave(nc.vector.tensor_copy, planes, s0, S - C, C)
         quantize(s0, n)
-        multiply(0, s0, n - C, 6)
-        multiply(0, S - C, C, 7, on_vector=True)
+        multiply(0, s0, n - C)
+        multiply(0, S - C, C, on_vector=True)
         for j in range(1, KT):
             for s0 in range(0, S, BANK):
-                multiply(j, s0, BANK, 5 + used % 3)
-                used += 1
+                multiply(j, s0, BANK)
 
         picked = {}
 
@@ -189,10 +182,10 @@ def tile_moe_bdx_lin_none_kernel(tc, dyT, w_words, w_scales, gate, offs, pos1, p
                 dst, picked[j, r][:, t : t + P], ident[:], start=(r == 0), stop=(r == terms - 1), is_transpose=True
             )
 
-        def turn_back(turned, groups, first_bank):
+        def turn_back(turned):
             sums = []
-            for g, (t0, t1) in enumerate(groups):
-                back = bank(first_bank + g)
+            for t0, t1 in TOKEN_GROUPS:
+                back = psum.tile([P, BANK], F32, name="bank")
                 for t in range(t0, t1, P):
                     nc.tensor.transpose(back[:, t - t0 : t - t0 + P], turned[:, t : t + P], ident[:])
                 sums.append(back)
@@ -207,33 +200,31 @@ def tile_moe_bdx_lin_none_kernel(tc, dyT, w_words, w_scales, gate, offs, pos1, p
             for r in range(TOP):
                 fetch(j, r)
             turned = keep.tile([P, T], F32, name="turned%d" % j)
-            for g, (t0, t1) in enumerate(TOKEN_GROUPS):
-                acc = bank(g)
+            for t0, t1 in TOKEN_GROUPS:
+                bank = psum.tile([P, BANK], F32, name="bank")
                 for t in range(t0, t1, P):
                     for r in range(TOP):
-                        turn_add(acc[:, t - t0 : t - t0 + P], j, r, t, TOP)
-                nc.scalar.copy(turned[:, t0:t1], acc[:, 0 : t1 - t0])
-            for (t0, t1), back in zip(TOKEN_GROUPS, turn_back(turned, TOKEN_GROUPS, 2)):
+                        turn_add(bank[:, t - t0 : t - t0 + P], j, r, t, TOP)
+                nc.scalar.copy(turned[:, t0:t1], bank[:, 0 : t1 - t0])
+            for (t0, t1), back in zip(TOKEN_GROUPS, turn_back(turned)):
                 nc.scalar.copy(result[j][:, t0:t1], back[:, 0 : t1 - t0])
             store(j, 0, T)
 
         j = KT - 1
-        blocks = list(range(0, T, P))
+        blocks = [t for t0, t1 in TOKEN_GROUPS for t in range(t0, t1, P)]
         turned = keep.tile([P, T], F32, name="turned%d" % j)
-        open_sums = {t: bank(b) for t, b in zip(blocks, (4, 5, 6, 7, 0))}
+        banks = {}
         for r in range(TOP - 1):
-            if r < TOP - 2:
-                fetch(j, r)
-            else:
-                fetch(j, r, 0, HALF)
-                fetch(j, r, HALF, T)
+            fetch(j, r)
             for t in blocks:
-                turn_add(open_sums[t][:, 0:P], j, r, t, TOP - 1)
+                if r == 0:
+                    banks[t] = psum.tile([P, BANK], F32, name="bank")
+                turn_add(banks[t][:, 0:P], j, r, t, TOP - 1)
         for t in blocks:
-            nc.scalar.copy(turned[:, t : t + P], open_sums[t][:, 0:P])
-        sums = turn_back(turned, LAST_GROUPS, 1)
-        fetch(j, TOP - 1, 0, HALF)
+            nc.scalar.copy(turned[:, t : t + P], banks[t][:, 0:P])
+        sums = turn_back(turned)
         fetch(j, TOP - 1, HALF, T)
-        for (t0, t1), back in zip(LAST_GROUPS, sums):
+        fetch(j, TOP - 1, 0, HALF)
+        for (t0, t1), back in zip(TOKEN_GROUPS, sums):
             nc.vector.tensor_tensor(result[j][:, t0:t1], back[:, 0 : t1 - t0], picked[j, TOP - 1][:, t0:t1], ADD)
             store(j, t0, t1)

@@ -1,7 +1,6 @@
 from contextlib import ExitStack
 
 import concourse.mybir as mybir
-from concourse.masks import make_identity
 
 K, T, E, C, N = 384, 640, 20, 128, 512
 TOP = 4
@@ -25,12 +24,12 @@ P = 128
 PACK = 4
 KT = K // P
 BANK = 512
-CHUNKS = (384, 896, 640, 384, 256)
+CHUNKS = (640, 1024, 512, 256, 128)
 WINDOW = max(T, max(CHUNKS) + 16)
-GATE_LOADS = (384, 896, 1280)
-W_LOADS = (6, 7, 7)
-TOKEN_GROUPS = ((384, 640), (0, 384))
+GATE_LOADS = (256, 384, 1024, 896)
+W_LOADS = (5, 8, 7)
 HALF = T // 2
+LAST_CUT = 384
 
 
 def starts(widths):
@@ -58,7 +57,8 @@ def tile_moe_bdx_lin_none_kernel(tc, dyT, w_words, w_scales, gate, offs, pos1, p
     with ExitStack() as ctx:
         lists = ctx.enter_context(tc.tile_pool(name="lists", bufs=1))
         keep = ctx.enter_context(tc.tile_pool(name="keep", bufs=1))
-        psum = ctx.enter_context(tc.psum_pool(name="psum", bufs=8))
+        ring = ctx.enter_context(tc.tile_pool(name="ring", bufs=2))
+        psum = ctx.enter_context(tc.psum_pool(name="psum", bufs=1))
 
         offs_sb = lists.tile([P, S // 16], U16, name="offs_sb")
         pos_sb = [lists.tile([P, T // 16], U16, name="pos_sb%d" % r) for r in range(TOP)]
@@ -66,16 +66,10 @@ def tile_moe_bdx_lin_none_kernel(tc, dyT, w_words, w_scales, gate, offs, pos1, p
         gate_sb = keep.tile([P, S], F32, name="gate_sb")
         w_sb = keep.tile([P, E, 2 * K], U8, name="w_sb", align_bytes=64)
         ws_sb = keep.tile([P, E, K], U8, name="ws_sb", align_bytes=64)
-        grouped = keep.tile([P, S, PACK], BF16, name="grouped", align_bytes=64)
-        g_codes = keep.tile([P, S], U32, name="g_codes", align_bytes=64)
-        g_scales = keep.tile([P, S], U8, name="g_scales", align_bytes=64)
         dx = [keep.tile([P, S], F32, name="dx%d" % j) for j in range(KT)]
-        ident = keep.tile([P, P], F32, name="ident")
 
-        if WINDOW > T:
-            for t in range(PACK):
-                nc.gpsimd.memset(dy[t][:, T:], 0.0)
-        make_identity(nc, ident[:])
+        for t in range(PACK):
+            nc.gpsimd.memset(dy[t][:, T:], 0.0)
         nc.vector.memset(ws_sb[:].bitcast(I32), 0)
 
         dy_rows = dyT.rearrange("(p t) j -> p t j", t=PACK)
@@ -85,146 +79,130 @@ def tile_moe_bdx_lin_none_kernel(tc, dyT, w_words, w_scales, gate, offs, pos1, p
             cols = slice(gate_at[i], gate_at[i] + GATE_LOADS[i])
             queue.dma_start(gate_sb[:, cols], gate[0:P, cols])
 
-        nc.sync.dma_start(offs_sb[:], offs)
-        nc.sync.dma_start(dy[0][:, 0:T], dy_rows[:, 0, :])
-        load_gate(0, nc.scalar)
-        for t in range(1, PACK):
-            nc.sync.dma_start(dy[t][:, 0:T], dy_rows[:, t, :])
-        for i in range(1, len(GATE_LOADS)):
-            load_gate(i, nc.sync)
-        for e0, ne in zip(starts(W_LOADS), W_LOADS):
+        def load_weights(i):
+            e0, ne = starts(W_LOADS)[i], W_LOADS[i]
             nc.sync.dma_start(
                 w_sb[:, e0 : e0 + ne, :].bitcast(I32),
                 w_words[e0 : e0 + ne, 0].rearrange("e p b -> p e b").bitcast(I32),
             )
+
+        nc.sync.dma_start(offs_sb[:], offs)
+        nc.sync.dma_start(dy[0][:, 0:T], dy_rows[:, 0, :])
+        load_gate(0, nc.sync)
+        load_gate(1, nc.sync)
+        for t in range(1, PACK):
+            nc.sync.dma_start(dy[t][:, 0:T], dy_rows[:, t, :])
+        load_gate(2, nc.sync)
+        load_gate(3, nc.sync)
         for q in range(4):
             nc.sync.dma_start(
                 ws_sb[32 * q : 32 * q + 4].bitcast(I32),
                 w_scales[:, 0, 4 * q : 4 * q + 4, :].rearrange("e r k -> r e k").bitcast(I32),
             )
+        load_weights(0)
+        for i in range(1, len(W_LOADS)):
+            load_weights(i)
         for r, pos in enumerate((pos1, pos2, pos3, pos4)):
             nc.sync.dma_start(pos_sb[r][:], pos)
 
         chunk_at = starts(CHUNKS)
+        grouped, g_codes, g_scales = {}, {}, {}
 
-        def gather(c):
+        def gather_and_interleave(c):
             s0, n = chunk_at[c], CHUNKS[c]
-            planes = keep.tile([P, PACK, n], F32, name="planes%d" % c)
+            planes = ring.tile([P, PACK, n], F32, name="planes")
             for t in range(PACK):
-                nc.vector.tensor_tensor(
-                    planes[:, t, :],
-                    dy[t][:].indirect(offs_sb[:, s0 // 16 : (s0 + n) // 16]),
-                    gate_sb[:, s0 : s0 + n],
-                    MULT,
+                cuts = zip(gate_at[:2], GATE_LOADS[:2]) if (c, t) == (0, 0) else [(s0, n)]
+                for s, m in cuts:
+                    nc.vector.tensor_tensor(
+                        planes[:, t, s - s0 : s - s0 + m],
+                        dy[t][:].indirect(offs_sb[:, s // 16 : (s + m) // 16]),
+                        gate_sb[:, s : s + m],
+                        MULT,
+                    )
+            tag = ("codes0", "scales0")[c - 2] if c in (2, 3) else "grouped%d" % c
+            grouped[c] = keep.tile([P, n, PACK], BF16, name="grouped%d" % c, tag=tag, align_bytes=64)
+            for s, m in halves(s0, n):
+                nc.scalar.copy(
+                    grouped[c][:, s - s0 : s - s0 + m, :].rearrange("p (a i) t -> p a t i", i=4),
+                    planes[:, :, s - s0 : s - s0 + m].rearrange("p t (a i) -> p a t i", i=4),
                 )
-            return planes
 
-        def interleave(copy, planes, s0, s, m):
-            copy(
-                grouped[:, s : s + m, :].rearrange("p (a i) t -> p a t i", i=4),
-                planes[:, :, s - s0 : s - s0 + m].rearrange("p t (a i) -> p a t i", i=4),
-            )
+        def quantize(c):
+            s0 = chunk_at[c]
+            g_codes[c] = keep.tile([P, CHUNKS[c]], U32, name="codes%d" % c, tag="codes%d" % c, align_bytes=64)
+            g_scales[c] = keep.tile([P, CHUNKS[c]], U8, name="scales%d" % c, tag="scales%d" % c, align_bytes=64)
+            for s, m in pieces(s0, CHUNKS[c]):
+                nc.vector.quantize_mx(
+                    out=g_codes[c][:, s - s0 : s - s0 + m].bitcast(FP8X4),
+                    scales=g_scales[c][:, s - s0 : s - s0 + m],
+                    in_=grouped[c][:, s - s0 : s - s0 + m, :].rearrange("p s t -> p (s t)"),
+                )
 
-        def quantize(s0, n):
-            nc.vector.quantize_mx(
-                out=g_codes[:, s0 : s0 + n].bitcast(FP8X4),
-                scales=g_scales[:, s0 : s0 + n],
-                in_=grouped[:, s0 : s0 + n, :].rearrange("p s t -> p (s t)"),
-            )
-
-        def multiply(j, s0, n, on_vector=False):
-            acc = psum.tile([P, BANK], F32, name="bank")
+        def multiply(j, s0, n, bank):
+            acc = psum.tile([P, BANK], F32, name="bank%d" % bank)
             for s in range(s0, s0 + n, C):
                 e = s // C
+                c = max(i for i in range(len(CHUNKS)) if chunk_at[i] <= s)
                 nc.tensor.matmul_mx(
                     out=acc[:, s - s0 : s - s0 + C],
                     lhsT=w_sb[:, e, 2 * P * j : 2 * P * (j + 1)].bitcast(FP4X4),
                     lhsT_scale=ws_sb[:, e, P * j : P * (j + 1)],
-                    rhs=g_codes[:, s : s + C].bitcast(FP8X4),
-                    rhs_scale=g_scales[:, s : s + C],
+                    rhs=g_codes[c][:, s - chunk_at[c] : s - chunk_at[c] + C].bitcast(FP8X4),
+                    rhs_scale=g_scales[c][:, s - chunk_at[c] : s - chunk_at[c] + C],
                     start=True,
                     stop=True,
                 )
-            if on_vector:
-                nc.vector.tensor_copy(dx[j][:, s0 : s0 + n], acc[:, 0:n])
+            return j, s0, n, acc
+
+        def empty(copy, j, s0, n, acc):
+            copy(dx[j][:, s0 : s0 + n], acc[:, 0:n])
+
+        def multiply_chunk(j, c, banks):
+            return [multiply(j, s, m, bank) for bank, (s, m) in zip(banks, halves(chunk_at[c], CHUNKS[c]))]
+
+        gather_and_interleave(0)
+        gather_and_interleave(1)
+        quantize(0)
+        for sums in multiply_chunk(0, 0, (0, 1)):
+            empty(nc.scalar.copy, *sums)
+        held = multiply_chunk(1, 0, (2, 3)) + multiply_chunk(2, 0, (4, 5))
+        gather_and_interleave(2)
+        quantize(1)
+        for sums in multiply_chunk(0, 1, (6, 7)):
+            empty(nc.scalar.copy, *sums)
+        gather_and_interleave(3)
+        gather_and_interleave(4)
+        for c in (2, 3, 4):
+            quantize(c)
+        for c, bank, copy in ((2, 0, nc.scalar.copy), (3, 1, nc.vector.tensor_copy), (4, 6, nc.vector.tensor_copy)):
+            for sums in multiply_chunk(0, c, (bank,)):
+                empty(copy, *sums)
+        for sums in held:
+            empty(nc.scalar.copy, *sums)
+        later = [cut for c in range(1, len(CHUNKS)) for cut in halves(chunk_at[c], CHUNKS[c])]
+        for i, (j, (s0, n)) in enumerate([(j, cut) for cut in later for j in range(1, KT)]):
+            empty(nc.scalar.copy, *multiply(j, s0, n, 2 + i % 4))
+
+        def fetch(j, r, partial, t0, t1):
+            total = keep.tile([P, t1 - t0], F32, name="sum%d_%d_%d" % (j, r, t0))
+            window = dx[j][:].indirect(pos_sb[r][:, t0 // 16 : t1 // 16])
+            if r == 0:
+                nc.vector.tensor_copy(total[:], window)
             else:
-                nc.scalar.copy(dx[j][:, s0 : s0 + n], acc[:, 0:n])
+                nc.vector.tensor_tensor(total[:], window, partial, ADD)
+            if r == TOP - 1:
+                nc.sync.dma_start(out[P * j : P * (j + 1), t0:t1], total[:])
+            return total[:]
 
-        last = len(CHUNKS) - 1
-        for c in range(len(CHUNKS)):
-            s0, n = chunk_at[c], CHUNKS[c]
-            planes = gather(c)
-            on_scalar = n if c < last else n - C
-            for s, m in halves(s0, on_scalar):
-                interleave(nc.scalar.copy, planes, s0, s, m)
-            if c > 0:
-                for s, m in pieces(chunk_at[c - 1], CHUNKS[c - 1]):
-                    quantize(s, m)
-                for s, m in halves(chunk_at[c - 1], CHUNKS[c - 1]):
-                    multiply(0, s, m)
-        interleave(nc.vector.tensor_copy, planes, s0, S - C, C)
-        quantize(s0, n)
-        multiply(0, s0, n - C)
-        multiply(0, S - C, C, on_vector=True)
-        for j in range(1, KT):
-            for s0 in range(0, S, BANK):
-                multiply(j, s0, BANK)
-
-        picked = {}
-
-        def fetch(j, r, t0=0, t1=T):
-            if (j, r) not in picked:
-                picked[j, r] = keep.tile([P, T], F32, name="picked%d_%d" % (j, r))
-            nc.vector.tensor_copy(picked[j, r][:, t0:t1], dx[j][:].indirect(pos_sb[r][:, t0 // 16 : t1 // 16]))
-
-        def turn_add(dst, j, r, t, terms):
-            nc.tensor.matmul(
-                dst, picked[j, r][:, t : t + P], ident[:], start=(r == 0), stop=(r == terms - 1), is_transpose=True
-            )
-
-        def turn_back(turned):
-            sums = []
-            for t0, t1 in TOKEN_GROUPS:
-                back = psum.tile([P, BANK], F32, name="bank")
-                for t in range(t0, t1, P):
-                    nc.tensor.transpose(back[:, t - t0 : t - t0 + P], turned[:, t : t + P], ident[:])
-                sums.append(back)
-            return sums
-
-        result = [keep.tile([P, T], F32, name="result%d" % j) for j in range(KT)]
-
-        def store(j, t0, t1):
-            nc.sync.dma_start(out[P * j : P * (j + 1), t0:t1], result[j][:, t0:t1])
-
-        for j in range(KT - 1):
-            for r in range(TOP):
-                fetch(j, r)
-            turned = keep.tile([P, T], F32, name="turned%d" % j)
-            for t0, t1 in TOKEN_GROUPS:
-                bank = psum.tile([P, BANK], F32, name="bank")
-                for t in range(t0, t1, P):
-                    for r in range(TOP):
-                        turn_add(bank[:, t - t0 : t - t0 + P], j, r, t, TOP)
-                nc.scalar.copy(turned[:, t0:t1], bank[:, 0 : t1 - t0])
-            for (t0, t1), back in zip(TOKEN_GROUPS, turn_back(turned)):
-                nc.scalar.copy(result[j][:, t0:t1], back[:, 0 : t1 - t0])
-            store(j, 0, T)
-
-        j = KT - 1
-        blocks = [t for t0, t1 in TOKEN_GROUPS for t in range(t0, t1, P)]
-        turned = keep.tile([P, T], F32, name="turned%d" % j)
-        banks = {}
+        low = high = None
+        for r in range(TOP):
+            low = fetch(0, r, low, 0, HALF)
+            high = fetch(0, r, high, HALF, T)
+        second = third = None
         for r in range(TOP - 1):
-            fetch(j, r)
-            for t in blocks:
-                if r == 0:
-                    banks[t] = psum.tile([P, BANK], F32, name="bank")
-                turn_add(banks[t][:, 0:P], j, r, t, TOP - 1)
-        for t in blocks:
-            nc.scalar.copy(turned[:, t : t + P], banks[t][:, 0:P])
-        sums = turn_back(turned)
-        fetch(j, TOP - 1, HALF, T)
-        fetch(j, TOP - 1, 0, HALF)
-        for (t0, t1), back in zip(TOKEN_GROUPS, sums):
-            nc.vector.tensor_tensor(result[j][:, t0:t1], back[:, 0 : t1 - t0], picked[j, TOP - 1][:, t0:t1], ADD)
-            store(j, t0, t1)
+            second = fetch(1, r, second, 0, T)
+            third = fetch(2, r, third, 0, T)
+        fetch(1, TOP - 1, second, 0, T)
+        fetch(2, TOP - 1, third[:, 0:LAST_CUT], 0, LAST_CUT)
+        fetch(2, TOP - 1, third[:, LAST_CUT:T], LAST_CUT, T)

@@ -1,6 +1,7 @@
 from contextlib import ExitStack
 
 import concourse.mybir as mybir
+from concourse.masks import make_identity
 
 K, T, E, C, N = 384, 640, 20, 128, 512
 TOP = 4
@@ -28,7 +29,6 @@ CHUNKS = (640, 1024, 512, 256, 128)
 WINDOW = max(T, max(CHUNKS) + 16)
 GATE_LOADS = (256, 384, 1024, 896)
 W_LOADS = (5, 8, 7)
-HALF = T // 2
 LAST_CUT = 384
 
 
@@ -38,7 +38,7 @@ def starts(widths):
 
 def pieces(s0, n):
     cut = []
-    for width in (512, 256, 128):
+    for width in (1024, 512, 256, 128):
         while n >= width:
             cut.append((s0, width))
             s0, n = s0 + width, n - width
@@ -68,8 +68,10 @@ def tile_moe_bdx_lin_none_kernel(tc, dyT, w_words, w_scales, gate, offs, pos1, p
         ws_sb = keep.tile([P, E, K], U8, name="ws_sb", align_bytes=64)
         dx = [keep.tile([P, S], F32, name="dx%d" % j) for j in range(KT)]
 
+        ident = keep.tile([P, P], F32, name="ident")
         for t in range(PACK):
             nc.gpsimd.memset(dy[t][:, T:], 0.0)
+        make_identity(nc, ident[:])
         nc.vector.memset(ws_sb[:].bitcast(I32), 0)
 
         dy_rows = dyT.rearrange("(p t) j -> p t j", t=PACK)
@@ -175,9 +177,13 @@ def tile_moe_bdx_lin_none_kernel(tc, dyT, w_words, w_scales, gate, offs, pos1, p
         gather_and_interleave(4)
         for c in (2, 3, 4):
             quantize(c)
-        for c, bank, copy in ((2, 0, nc.scalar.copy), (3, 1, nc.vector.tensor_copy), (4, 6, nc.vector.tensor_copy)):
-            for sums in multiply_chunk(0, c, (bank,)):
-                empty(copy, *sums)
+        for s0, n, bank, copy in (
+            (chunk_at[2], 256, 0, nc.scalar.copy),
+            (chunk_at[2] + 256, 256, 1, nc.scalar.copy),
+            (chunk_at[3], 256, 6, nc.scalar.copy),
+            (chunk_at[4], 128, 7, nc.vector.tensor_copy),
+        ):
+            empty(copy, *multiply(0, s0, n, bank))
         for sums in held:
             empty(nc.scalar.copy, *sums)
         later = [cut for c in range(1, len(CHUNKS)) for cut in halves(chunk_at[c], CHUNKS[c])]
@@ -195,10 +201,30 @@ def tile_moe_bdx_lin_none_kernel(tc, dyT, w_words, w_scales, gate, offs, pos1, p
                 nc.sync.dma_start(out[P * j : P * (j + 1), t0:t1], total[:])
             return total[:]
 
-        low = high = None
+        picked = [keep.tile([P, T], F32, name="picked%d" % r) for r in range(TOP)]
         for r in range(TOP):
-            low = fetch(0, r, low, 0, HALF)
-            high = fetch(0, r, high, HALF, T)
+            nc.vector.tensor_copy(picked[r][:], dx[0][:].indirect(pos_sb[r][:]))
+        turned = keep.tile([P, T], F32, name="turned")
+        result = keep.tile([P, T], F32, name="result")
+        for bank, (t0, n) in zip((2, 3), halves(0, T)):
+            acc = psum.tile([P, BANK], F32, name="bank%d" % bank)
+            for t in range(t0, t0 + n, P):
+                for r in range(TOP):
+                    nc.tensor.matmul(
+                        acc[:, t - t0 : t - t0 + P],
+                        picked[r][:, t : t + P],
+                        ident[:],
+                        start=(r == 0),
+                        stop=(r == TOP - 1),
+                        is_transpose=True,
+                    )
+            nc.scalar.copy(turned[:, t0 : t0 + n], acc[:, 0:n])
+        for bank, (t0, n) in zip((0, 1), halves(0, T)):
+            acc = psum.tile([P, BANK], F32, name="bank%d" % bank)
+            for t in range(t0, t0 + n, P):
+                nc.tensor.transpose(acc[:, t - t0 : t - t0 + P], turned[:, t : t + P], ident[:])
+            nc.scalar.copy(result[:, t0 : t0 + n], acc[:, 0:n])
+        nc.scalar.dma_start(out[0:P, :], result[:])
         second = third = None
         for r in range(TOP - 1):
             second = fetch(1, r, second, 0, T)

@@ -52,6 +52,10 @@ def halves(s0, n):
     return [(s0, first), (s0 + first, n - first)]
 
 
+def in_two(s0, n):
+    return [(s0, n // 2), (s0 + n // 2, n // 2)]
+
+
 def tile_moe_bdx_lin_none_kernel(tc, dyT, w_words, w_scales, gate, offs, pos1, pos2, pos3, pos4, out):
     nc = tc.nc
     with ExitStack() as ctx:
@@ -69,8 +73,6 @@ def tile_moe_bdx_lin_none_kernel(tc, dyT, w_words, w_scales, gate, offs, pos1, p
         dx = [keep.tile([P, S], F32, name="dx%d" % j) for j in range(KT)]
 
         ident = keep.tile([P, P], F32, name="ident")
-        for t in range(PACK):
-            nc.gpsimd.memset(dy[t][:, T:], 0.0)
         make_identity(nc, ident[:])
         nc.vector.memset(ws_sb[:].bitcast(I32), 0)
 
@@ -134,7 +136,7 @@ def tile_moe_bdx_lin_none_kernel(tc, dyT, w_words, w_scales, gate, offs, pos1, p
             s0 = chunk_at[c]
             g_codes[c] = keep.tile([P, CHUNKS[c]], U32, name="codes%d" % c, tag="codes%d" % c, align_bytes=64)
             g_scales[c] = keep.tile([P, CHUNKS[c]], U8, name="scales%d" % c, tag="scales%d" % c, align_bytes=64)
-            for s, m in pieces(s0, CHUNKS[c]):
+            for s, m in in_two(s0, CHUNKS[c]) if c == 2 else pieces(s0, CHUNKS[c]):
                 nc.vector.quantize_mx(
                     out=g_codes[c][:, s - s0 : s - s0 + m].bitcast(FP8X4),
                     scales=g_scales[c][:, s - s0 : s - s0 + m],
@@ -181,7 +183,7 @@ def tile_moe_bdx_lin_none_kernel(tc, dyT, w_words, w_scales, gate, offs, pos1, p
             (chunk_at[2], 256, 0, nc.scalar.copy),
             (chunk_at[2] + 256, 256, 1, nc.scalar.copy),
             (chunk_at[3], 256, 6, nc.scalar.copy),
-            (chunk_at[4], 128, 7, nc.vector.tensor_copy),
+            (chunk_at[4], 128, 7, nc.scalar.copy),
         ):
             empty(copy, *multiply(0, s0, n, bank))
         for sums in held:

@@ -30,6 +30,7 @@ WINDOW = max(T, max(CHUNKS) + 16)
 GATE_LOADS = (256, 384, 1024, 896)
 W_LOADS = (5, 8, 7)
 LAST_CUT = 384
+HEAD_START = {1: 384, 2: 192}
 
 
 def starts(widths):
@@ -115,8 +116,12 @@ def tile_moe_bdx_lin_none_kernel(tc, dyT, w_words, w_scales, gate, offs, pos1, p
         def gather_and_interleave(c):
             s0, n = chunk_at[c], CHUNKS[c]
             planes = ring.tile([P, PACK, n], F32, name="planes")
+            first = HEAD_START.get(c)
+            copies = [(s0, first), (s0 + first, n - first)] if first else halves(s0, n)
             for t in range(PACK):
                 cuts = zip(gate_at[:2], GATE_LOADS[:2]) if (c, t) == (0, 0) else [(s0, n)]
+                if c in HEAD_START and t == PACK - 1:
+                    cuts = copies
                 for s, m in cuts:
                     nc.vector.tensor_tensor(
                         planes[:, t, s - s0 : s - s0 + m],
@@ -126,7 +131,7 @@ def tile_moe_bdx_lin_none_kernel(tc, dyT, w_words, w_scales, gate, offs, pos1, p
                     )
             tag = ("codes0", "scales0")[c - 2] if c in (2, 3) else "grouped%d" % c
             grouped[c] = keep.tile([P, n, PACK], BF16, name="grouped%d" % c, tag=tag, align_bytes=64)
-            for s, m in halves(s0, n):
+            for s, m in copies:
                 nc.scalar.copy(
                     grouped[c][:, s - s0 : s - s0 + m, :].rearrange("p (a i) t -> p a t i", i=4),
                     planes[:, :, s - s0 : s - s0 + m].rearrange("p t (a i) -> p a t i", i=4),

@@ -29,7 +29,7 @@ CHUNKS = (640, 1024, 512, 256, 128)
 WINDOW = max(T, max(CHUNKS) + 16)
 GATE_LOADS = (256, 384, 1024, 896)
 W_LOADS = (5, 8, 7)
-LAST_CUT = 384
+LAST_CUTS = (352, 192, 96)
 HEAD_START = {1: 384, 2: 192}
 
 
@@ -69,6 +69,11 @@ def tile_moe_bdx_lin_none_kernel(tc, dyT, w_words, w_scales, gate, offs, pos1, p
         pos_sb = [lists.tile([P, T // 16], U16, name="pos_sb%d" % r) for r in range(TOP)]
         dy = [keep.tile([P, WINDOW], F32, name="dy%d" % t) for t in range(PACK)]
         gate_sb = keep.tile([P, S], F32, name="gate_sb")
+        first_cuts = [(starts(CHUNKS)[c] // C, CHUNKS[c] // C) for c in range(2)]
+        w_first = [
+            keep.tile([P, ne, 2 * P], U8, name="w_first%d" % i, tag="w_first%d" % i, align_bytes=64)
+            for i, (e0, ne) in enumerate(first_cuts)
+        ]
         w_sb = keep.tile([P, E, 2 * K], U8, name="w_sb", align_bytes=64)
         ws_sb = keep.tile([P, E, K], U8, name="ws_sb", align_bytes=64)
         dx = [keep.tile([P, S], F32, name="dx%d" % j) for j in range(KT)]
@@ -99,14 +104,22 @@ def tile_moe_bdx_lin_none_kernel(tc, dyT, w_words, w_scales, gate, offs, pos1, p
             nc.sync.dma_start(dy[t][:, 0:T], dy_rows[:, t, :])
         load_gate(2, nc.sync)
         load_gate(3, nc.sync)
+        for (e0, ne), tile in zip(first_cuts, w_first):
+            nc.sync.dma_start(
+                tile[:].bitcast(I32),
+                w_words[e0 : e0 + ne, 0, :, 0 : 2 * P].rearrange("e p b -> p e b").bitcast(I32),
+            )
+        early = starts(W_LOADS)[2]
+        nc.sync.dma_start(
+            w_sb[:, 0:early, 2 * P :].bitcast(I32),
+            w_words[0:early, 0, :, 2 * P :].rearrange("e p b -> p e b").bitcast(I32),
+        )
+        load_weights(2)
         for q in range(4):
             nc.sync.dma_start(
                 ws_sb[32 * q : 32 * q + 4].bitcast(I32),
                 w_scales[:, 0, 4 * q : 4 * q + 4, :].rearrange("e r k -> r e k").bitcast(I32),
             )
-        load_weights(0)
-        for i in range(1, len(W_LOADS)):
-            load_weights(i)
         for r, pos in enumerate((pos1, pos2, pos3, pos4)):
             nc.sync.dma_start(pos_sb[r][:], pos)
 
@@ -129,7 +142,7 @@ def tile_moe_bdx_lin_none_kernel(tc, dyT, w_words, w_scales, gate, offs, pos1, p
                         gate_sb[:, s : s + m],
                         MULT,
                     )
-            tag = ("codes0", "scales0")[c - 2] if c in (2, 3) else "grouped%d" % c
+            tag = ("w_first0", "w_first1")[c - 2] if c in (2, 3) else "grouped%d" % c
             grouped[c] = keep.tile([P, n, PACK], BF16, name="grouped%d" % c, tag=tag, align_bytes=64)
             for s, m in copies:
                 nc.scalar.copy(
@@ -153,9 +166,12 @@ def tile_moe_bdx_lin_none_kernel(tc, dyT, w_words, w_scales, gate, offs, pos1, p
             for s in range(s0, s0 + n, C):
                 e = s // C
                 c = max(i for i in range(len(CHUNKS)) if chunk_at[i] <= s)
+                words = w_sb[:, e, 2 * P * j : 2 * P * (j + 1)]
+                if j == 0 and c < len(first_cuts):
+                    words = w_first[c][:, e - first_cuts[c][0], :]
                 nc.tensor.matmul_mx(
                     out=acc[:, s - s0 : s - s0 + C],
-                    lhsT=w_sb[:, e, 2 * P * j : 2 * P * (j + 1)].bitcast(FP4X4),
+                    lhsT=words.bitcast(FP4X4),
                     lhsT_scale=ws_sb[:, e, P * j : P * (j + 1)],
                     rhs=g_codes[c][:, s - chunk_at[c] : s - chunk_at[c] + C].bitcast(FP8X4),
                     rhs_scale=g_scales[c][:, s - chunk_at[c] : s - chunk_at[c] + C],
@@ -175,11 +191,11 @@ def tile_moe_bdx_lin_none_kernel(tc, dyT, w_words, w_scales, gate, offs, pos1, p
         quantize(0)
         for sums in multiply_chunk(0, 0, (0, 1)):
             empty(nc.scalar.copy, *sums)
-        held = multiply_chunk(1, 0, (2, 3)) + multiply_chunk(2, 0, (4, 5))
         gather_and_interleave(2)
         quantize(1)
         for sums in multiply_chunk(0, 1, (6, 7)):
             empty(nc.scalar.copy, *sums)
+        held = multiply_chunk(1, 1, (2, 3)) + multiply_chunk(2, 1, (4, 5))
         gather_and_interleave(3)
         gather_and_interleave(4)
         for c in (2, 3, 4):
@@ -193,7 +209,7 @@ def tile_moe_bdx_lin_none_kernel(tc, dyT, w_words, w_scales, gate, offs, pos1, p
             empty(copy, *multiply(0, s0, n, bank))
         for sums in held:
             empty(nc.scalar.copy, *sums)
-        later = [cut for c in range(1, len(CHUNKS)) for cut in halves(chunk_at[c], CHUNKS[c])]
+        later = [cut for c in (0, 2, 3, 4) for cut in halves(chunk_at[c], CHUNKS[c])]
         for i, (j, (s0, n)) in enumerate([(j, cut) for cut in later for j in range(1, KT)]):
             empty(nc.scalar.copy, *multiply(j, s0, n, 2 + i % 4))
 
@@ -237,5 +253,5 @@ def tile_moe_bdx_lin_none_kernel(tc, dyT, w_words, w_scales, gate, offs, pos1, p
             second = fetch(1, r, second, 0, T)
             third = fetch(2, r, third, 0, T)
         fetch(1, TOP - 1, second, 0, T)
-        fetch(2, TOP - 1, third[:, 0:LAST_CUT], 0, LAST_CUT)
-        fetch(2, TOP - 1, third[:, LAST_CUT:T], LAST_CUT, T)
+        for t0, n in zip(starts(LAST_CUTS), LAST_CUTS):
+            fetch(2, TOP - 1, third[:, t0 : t0 + n], t0, t0 + n)

@@ -27,9 +27,10 @@ KT = K // P
 BANK = 512
 CHUNKS = (640, 1024, 512, 256, 128)
 WINDOW = max(T, max(CHUNKS) + 16)
-GATE_LOADS = (256, 384, 1024, 896)
+GATE_LOADS = (640, 1024, 896)
 W_LOADS = (5, 8, 7)
 LAST_CUTS = (352, 192, 96)
+BARE = 2
 HEAD_START = {1: 384, 2: 192}
 
 
@@ -98,12 +99,12 @@ def tile_moe_bdx_lin_none_kernel(tc, dyT, w_words, w_scales, gate, offs, pos1, p
 
         nc.sync.dma_start(offs_sb[:], offs)
         nc.sync.dma_start(dy[0][:, 0:T], dy_rows[:, 0, :])
-        load_gate(0, nc.sync)
-        load_gate(1, nc.sync)
         for t in range(1, PACK):
+            if t == BARE:
+                load_gate(0, nc.sync)
             nc.sync.dma_start(dy[t][:, 0:T], dy_rows[:, t, :])
+        load_gate(1, nc.sync)
         load_gate(2, nc.sync)
-        load_gate(3, nc.sync)
         for (e0, ne), tile in zip(first_cuts, w_first):
             nc.sync.dma_start(
                 tile[:].bitcast(I32),
@@ -126,15 +127,45 @@ def tile_moe_bdx_lin_none_kernel(tc, dyT, w_words, w_scales, gate, offs, pos1, p
         chunk_at = starts(CHUNKS)
         grouped, g_codes, g_scales = {}, {}, {}
 
+        def turn(source, n, bank):
+            acc = psum.tile([P, BANK], F32, name="bank%d" % bank)
+            for s in range(0, n, P):
+                nc.tensor.transpose(acc[:, s : s + P], source[:, s : s + P], ident[:])
+            return acc
+
+        n0 = CHUNKS[0]
+        gate_col = keep.tile([P, n0 // P], F32, name="gate_col")
+        for i, (s, m) in enumerate(halves(0, n0)):
+            nc.scalar.copy(gate_col[:, s // P : (s + m) // P], turn(gate_sb[:, s : s + m], m, i)[:, 0:m:P])
+
+        def gather_without_gate(t, plane):
+            bare = keep.tile([P, n0], F32, name="bare%d" % t)
+            nc.vector.tensor_copy(bare[:], dy[t][:].indirect(offs_sb[:, 0 : n0 // 16]))
+            gated = keep.tile([P, n0], F32, name="gated%d" % t)
+            for i, (s, m) in enumerate(halves(0, n0)):
+                acc = turn(bare[:, s : s + m], m, 2 + 4 * t + i)
+                for b in range(m // P):
+                    nc.scalar.activation(
+                        gated[:, s + P * b : s + P * (b + 1)],
+                        acc[:, P * b : P * (b + 1)],
+                        mybir.ActivationFunctionType.Copy,
+                        scale=gate_col[:, s // P + b : s // P + b + 1],
+                    )
+            for i, (s, m) in enumerate(halves(0, n0)):
+                nc.scalar.copy(plane[:, s : s + m], turn(gated[:, s : s + m], m, 4 - 4 * t + i)[:, 0:m])
+
         def gather_and_interleave(c):
             s0, n = chunk_at[c], CHUNKS[c]
             planes = ring.tile([P, PACK, n], F32, name="planes")
             first = HEAD_START.get(c)
             copies = [(s0, first), (s0 + first, n - first)] if first else halves(s0, n)
             for t in range(PACK):
-                cuts = zip(gate_at[:2], GATE_LOADS[:2]) if (c, t) == (0, 0) else [(s0, n)]
+                cuts = [(s0, n)]
                 if c in HEAD_START and t == PACK - 1:
                     cuts = copies
+                if c == 0 and t < BARE:
+                    gather_without_gate(t, planes[:, t, :])
+                    continue
                 for s, m in cuts:
                     nc.vector.tensor_tensor(
                         planes[:, t, s - s0 : s - s0 + m],

@@ -110,17 +110,17 @@ def tile_moe_bdx_lin_none_kernel(tc, dyT, w_words, w_scales, gate, offs, pos1, p
                 tile[:].bitcast(I32),
                 w_words[e0 : e0 + ne, 0, :, 0 : 2 * P].rearrange("e p b -> p e b").bitcast(I32),
             )
+        for r in range(4):
+            nc.sync.dma_start(
+                ws_sb[r:P:32].bitcast(I32),
+                w_scales[:, 0, r:16:4, :].rearrange("e q k -> q e k").bitcast(I32),
+            )
         early = starts(W_LOADS)[2]
         nc.sync.dma_start(
             w_sb[:, 0:early, 2 * P :].bitcast(I32),
             w_words[0:early, 0, :, 2 * P :].rearrange("e p b -> p e b").bitcast(I32),
         )
         load_weights(2)
-        for q in range(4):
-            nc.sync.dma_start(
-                ws_sb[32 * q : 32 * q + 4].bitcast(I32),
-                w_scales[:, 0, 4 * q : 4 * q + 4, :].rearrange("e r k -> r e k").bitcast(I32),
-            )
         for r, pos in enumerate((pos1, pos2, pos3, pos4)):
             nc.sync.dma_start(pos_sb[r][:], pos)
 
@@ -240,7 +240,7 @@ def tile_moe_bdx_lin_none_kernel(tc, dyT, w_words, w_scales, gate, offs, pos1, p
             empty(copy, *multiply(0, s0, n, bank))
         for sums in held:
             empty(nc.scalar.copy, *sums)
-        later = [cut for c in (0, 2, 3, 4) for cut in halves(chunk_at[c], CHUNKS[c])]
+        later = [cut for c in (4, 3, 0, 2) for cut in halves(chunk_at[c], CHUNKS[c])]
         for i, (j, (s0, n)) in enumerate([(j, cut) for cut in later for j in range(1, KT)]):
             empty(nc.scalar.copy, *multiply(j, s0, n, 2 + i % 4))
 

@@ -26,25 +26,15 @@ PACK = 4
 KT = K // P
 BANK = 512
 CHUNKS = (640, 1024, 512, 256, 128)
-WINDOW = max(T, max(CHUNKS) + 16)
-GATE_LOADS = (640, 1024, 896)
-W_LOADS = (5, 8, 7)
+WINDOW = max(CHUNKS) + 16
+PLANES_AT = (0, 16384, 8192, 16384, 8192)
+HEAD_START = {1: 384, 2: 192}
 LAST_CUTS = (352, 192, 96)
 BARE = 2
-HEAD_START = {1: 384, 2: 192}
 
 
 def starts(widths):
     return [sum(widths[:i]) for i in range(len(widths))]
-
-
-def pieces(s0, n):
-    cut = []
-    for width in (1024, 512, 256, 128):
-        while n >= width:
-            cut.append((s0, width))
-            s0, n = s0 + width, n - width
-    return cut
 
 
 def halves(s0, n):
@@ -54,96 +44,94 @@ def halves(s0, n):
     return [(s0, first), (s0 + first, n - first)]
 
 
-def in_two(s0, n):
-    return [(s0, n // 2), (s0 + n // 2, n // 2)]
-
-
 def tile_moe_bdx_lin_none_kernel(tc, dyT, w_words, w_scales, gate, offs, pos1, pos2, pos3, pos4, out):
     nc = tc.nc
     with ExitStack() as ctx:
         lists = ctx.enter_context(tc.tile_pool(name="lists", bufs=1))
         keep = ctx.enter_context(tc.tile_pool(name="keep", bufs=1))
-        ring = ctx.enter_context(tc.tile_pool(name="ring", bufs=2))
+        placed = ctx.enter_context(tc.tile_pool(name="placed", bufs=1))
         psum = ctx.enter_context(tc.psum_pool(name="psum", bufs=1))
 
+        chunk_at = starts(CHUNKS)
         offs_sb = lists.tile([P, S // 16], U16, name="offs_sb")
         pos_sb = [lists.tile([P, T // 16], U16, name="pos_sb%d" % r) for r in range(TOP)]
         dy = [keep.tile([P, WINDOW], F32, name="dy%d" % t) for t in range(PACK)]
-        gate_sb = keep.tile([P, S], F32, name="gate_sb")
-        first_cuts = [(starts(CHUNKS)[c] // C, CHUNKS[c] // C) for c in range(2)]
+        first_experts = [(chunk_at[c] // C, CHUNKS[c] // C) for c in range(2)]
         w_first = [
-            keep.tile([P, ne, 2 * P], U8, name="w_first%d" % i, tag="w_first%d" % i, align_bytes=64)
-            for i, (e0, ne) in enumerate(first_cuts)
+            keep.tile([P, ne, 2 * P], U8, name="w_first%d" % c, tag="w_first%d" % c, align_bytes=64)
+            for c, (e0, ne) in enumerate(first_experts)
         ]
         w_sb = keep.tile([P, E, 2 * K], U8, name="w_sb", align_bytes=64)
         ws_sb = keep.tile([P, E, K], U8, name="ws_sb", align_bytes=64)
         dx = [keep.tile([P, S], F32, name="dx%d" % j) for j in range(KT)]
 
+        gate_rows = keep.tile([P, P], F32, name="gate_rows")
+        row0 = 32 - E
+        by_expert = gate[0].rearrange("(e c) -> e c", c=C)
+        nc.scalar.dma_start(gate_rows[row0 : row0 + 16, :], by_expert[0:16])
+        nc.scalar.dma_start(gate_rows[row0 + 16 : 32, :], by_expert[16:E])
+        for p0, p1 in ((0, row0), (32, 64), (64, P)):
+            nc.gpsimd.memset(gate_rows[p0:p1, :], 0.0)
         ident = keep.tile([P, P], F32, name="ident")
         make_identity(nc, ident[:])
         nc.vector.memset(ws_sb[:].bitcast(I32), 0)
 
         dy_rows = dyT.rearrange("(p t) j -> p t j", t=PACK)
-        gate_at = starts(GATE_LOADS)
-
-        def load_gate(i, queue):
-            cols = slice(gate_at[i], gate_at[i] + GATE_LOADS[i])
-            queue.dma_start(gate_sb[:, cols], gate[0:P, cols])
-
-        def load_weights(i):
-            e0, ne = starts(W_LOADS)[i], W_LOADS[i]
-            nc.sync.dma_start(
-                w_sb[:, e0 : e0 + ne, :].bitcast(I32),
-                w_words[e0 : e0 + ne, 0].rearrange("e p b -> p e b").bitcast(I32),
-            )
-
         nc.sync.dma_start(offs_sb[:], offs)
-        nc.sync.dma_start(dy[0][:, 0:T], dy_rows[:, 0, :])
-        for t in range(1, PACK):
-            if t == BARE:
-                load_gate(0, nc.sync)
+        for t in range(PACK):
             nc.sync.dma_start(dy[t][:, 0:T], dy_rows[:, t, :])
-        load_gate(1, nc.sync)
-        load_gate(2, nc.sync)
-        for (e0, ne), tile in zip(first_cuts, w_first):
+        for (e0, ne), tile in zip(first_experts, w_first):
             nc.sync.dma_start(
                 tile[:].bitcast(I32),
                 w_words[e0 : e0 + ne, 0, :, 0 : 2 * P].rearrange("e p b -> p e b").bitcast(I32),
             )
+        early = sum(first_experts[-1])
+        nc.sync.dma_start(
+            w_sb[:, 0:early, 2 * P :].bitcast(I32),
+            w_words[0:early, 0, :, 2 * P :].rearrange("e p b -> p e b").bitcast(I32),
+        )
+        nc.sync.dma_start(
+            w_sb[:, early:, :].bitcast(I32),
+            w_words[early:, 0].rearrange("e p b -> p e b").bitcast(I32),
+        )
         for r in range(4):
             nc.sync.dma_start(
                 ws_sb[r:P:32].bitcast(I32),
                 w_scales[:, 0, r:16:4, :].rearrange("e q k -> q e k").bitcast(I32),
             )
-        early = starts(W_LOADS)[2]
-        nc.sync.dma_start(
-            w_sb[:, 0:early, 2 * P :].bitcast(I32),
-            w_words[0:early, 0, :, 2 * P :].rearrange("e p b -> p e b").bitcast(I32),
-        )
-        load_weights(2)
         for r, pos in enumerate((pos1, pos2, pos3, pos4)):
             nc.sync.dma_start(pos_sb[r][:], pos)
 
-        chunk_at = starts(CHUNKS)
-        grouped, g_codes, g_scales = {}, {}, {}
-
-        def turn(source, n, bank):
+        def turn(blocks, bank):
             acc = psum.tile([P, BANK], F32, name="bank%d" % bank)
-            for s in range(0, n, P):
-                nc.tensor.transpose(acc[:, s : s + P], source[:, s : s + P], ident[:])
+            for i, block in enumerate(blocks):
+                nc.tensor.transpose(acc[:, P * i : P * (i + 1)], block, ident[:])
             return acc
 
-        n0 = CHUNKS[0]
-        gate_col = keep.tile([P, n0 // P], F32, name="gate_col")
-        for i, (s, m) in enumerate(halves(0, n0)):
-            nc.scalar.copy(gate_col[:, s // P : (s + m) // P], turn(gate_sb[:, s : s + m], m, i)[:, 0:m:P])
+        def blocks_of(tile, s, m):
+            return [tile[:, b : b + P] for b in range(s, s + m, P)]
+
+        gate_col = keep.tile([P, E], F32, name="gate_col")
+        nc.scalar.copy(gate_col[:], turn([gate_rows[:]], 0)[:, row0:32])
+        gate_sb = keep.tile([P, S], F32, name="gate_sb")
+
+        def spread_gate(s0, n, banks):
+            for bank, (s, m) in zip(banks, halves(s0, n)):
+                columns = [gate_col[:, e : e + 1].to_broadcast([P, P]) for e in range(s // C, (s + m) // C)]
+                nc.scalar.copy(gate_sb[:, s : s + m], turn(columns, bank)[:, 0:m])
+
+        spread_gate(chunk_at[0], CHUNKS[0], (1, 2))
+        spread_gate(chunk_at[1], CHUNKS[1], (3, 0))
+
+        grouped, g_codes, g_scales = {}, {}, {}
 
         def gather_without_gate(t, plane):
+            n0 = CHUNKS[0]
             bare = keep.tile([P, n0], F32, name="bare%d" % t)
             nc.vector.tensor_copy(bare[:], dy[t][:].indirect(offs_sb[:, 0 : n0 // 16]))
             gated = keep.tile([P, n0], F32, name="gated%d" % t)
             for i, (s, m) in enumerate(halves(0, n0)):
-                acc = turn(bare[:, s : s + m], m, 2 + 4 * t + i)
+                acc = turn(blocks_of(bare, s, m), (1, 2, 3, 0)[2 * t + i])
                 for b in range(m // P):
                     nc.scalar.activation(
                         gated[:, s + P * b : s + P * (b + 1)],
@@ -152,44 +140,43 @@ def tile_moe_bdx_lin_none_kernel(tc, dyT, w_words, w_scales, gate, offs, pos1, p
                         scale=gate_col[:, s // P + b : s // P + b + 1],
                     )
             for i, (s, m) in enumerate(halves(0, n0)):
-                nc.scalar.copy(plane[:, s : s + m], turn(gated[:, s : s + m], m, 4 - 4 * t + i)[:, 0:m])
+                nc.scalar.copy(plane[:, s : s + m], turn(blocks_of(gated, s, m), 4 + 2 * t + i)[:, 0:m])
 
         def gather_and_interleave(c):
             s0, n = chunk_at[c], CHUNKS[c]
-            planes = ring.tile([P, PACK, n], F32, name="planes")
+            planes = placed.tile([P, PACK, n], F32, name="planes%d" % c, offset=PLANES_AT[c], align_bytes=64)
             first = HEAD_START.get(c)
             copies = [(s0, first), (s0 + first, n - first)] if first else halves(s0, n)
             for t in range(PACK):
-                cuts = [(s0, n)]
-                if c in HEAD_START and t == PACK - 1:
-                    cuts = copies
                 if c == 0 and t < BARE:
                     gather_without_gate(t, planes[:, t, :])
                     continue
-                for s, m in cuts:
+                for s, m in copies if first and t == PACK - 1 else [(s0, n)]:
                     nc.vector.tensor_tensor(
                         planes[:, t, s - s0 : s - s0 + m],
                         dy[t][:].indirect(offs_sb[:, s // 16 : (s + m) // 16]),
                         gate_sb[:, s : s + m],
                         MULT,
                     )
-            tag = ("w_first0", "w_first1")[c - 2] if c in (2, 3) else "grouped%d" % c
-            grouped[c] = keep.tile([P, n, PACK], BF16, name="grouped%d" % c, tag=tag, align_bytes=64)
+            if c == 1:
+                grouped[c] = placed.tile([P, n, PACK], BF16, name="grouped1", offset=0, align_bytes=64)
+            else:
+                tag = "w_first%d" % (c - 2) if c in (2, 3) else "grouped%d" % c
+                grouped[c] = keep.tile([P, n, PACK], BF16, name="grouped%d" % c, tag=tag, align_bytes=64)
             for s, m in copies:
                 nc.scalar.copy(
                     grouped[c][:, s - s0 : s - s0 + m, :].rearrange("p (a i) t -> p a t i", i=4),
                     planes[:, :, s - s0 : s - s0 + m].rearrange("p t (a i) -> p a t i", i=4),
                 )
 
-        def quantize(c):
-            s0 = chunk_at[c]
-            g_codes[c] = keep.tile([P, CHUNKS[c]], U32, name="codes%d" % c, tag="codes%d" % c, align_bytes=64)
-            g_scales[c] = keep.tile([P, CHUNKS[c]], U8, name="scales%d" % c, tag="scales%d" % c, align_bytes=64)
-            for s, m in in_two(s0, CHUNKS[c]) if c == 2 else pieces(s0, CHUNKS[c]):
+        def quantize(c, widths):
+            g_codes[c] = keep.tile([P, CHUNKS[c]], U32, name="codes%d" % c, align_bytes=64)
+            g_scales[c] = keep.tile([P, CHUNKS[c]], U8, name="scales%d" % c, align_bytes=64)
+            for s, m in zip(starts(widths), widths):
                 nc.vector.quantize_mx(
-                    out=g_codes[c][:, s - s0 : s - s0 + m].bitcast(FP8X4),
-                    scales=g_scales[c][:, s - s0 : s - s0 + m],
-                    in_=grouped[c][:, s - s0 : s - s0 + m, :].rearrange("p s t -> p (s t)"),
+                    out=g_codes[c][:, s : s + m].bitcast(FP8X4),
+                    scales=g_scales[c][:, s : s + m],
+                    in_=grouped[c][:, s : s + m, :].rearrange("p s t -> p (s t)"),
                 )
 
         def multiply(j, s0, n, bank):
@@ -198,91 +185,69 @@ def tile_moe_bdx_lin_none_kernel(tc, dyT, w_words, w_scales, gate, offs, pos1, p
                 e = s // C
                 c = max(i for i in range(len(CHUNKS)) if chunk_at[i] <= s)
                 words = w_sb[:, e, 2 * P * j : 2 * P * (j + 1)]
-                if j == 0 and c < len(first_cuts):
-                    words = w_first[c][:, e - first_cuts[c][0], :]
+                if j == 0 and e < early:
+                    words = w_first[c][:, e - first_experts[c][0], :]
+                cols = slice(s - chunk_at[c], s - chunk_at[c] + C)
                 nc.tensor.matmul_mx(
                     out=acc[:, s - s0 : s - s0 + C],
                     lhsT=words.bitcast(FP4X4),
                     lhsT_scale=ws_sb[:, e, P * j : P * (j + 1)],
-                    rhs=g_codes[c][:, s - chunk_at[c] : s - chunk_at[c] + C].bitcast(FP8X4),
-                    rhs_scale=g_scales[c][:, s - chunk_at[c] : s - chunk_at[c] + C],
+                    rhs=g_codes[c][:, cols].bitcast(FP8X4),
+                    rhs_scale=g_scales[c][:, cols],
                     start=True,
                     stop=True,
                 )
             return j, s0, n, acc
 
-        def empty(copy, j, s0, n, acc):
-            copy(dx[j][:, s0 : s0 + n], acc[:, 0:n])
+        def empty(j, s0, n, acc):
+            nc.scalar.copy(dx[j][:, s0 : s0 + n], acc[:, 0:n])
 
         def multiply_chunk(j, c, banks):
             return [multiply(j, s, m, bank) for bank, (s, m) in zip(banks, halves(chunk_at[c], CHUNKS[c]))]
 
         gather_and_interleave(0)
+        spread_gate(chunk_at[2], S - chunk_at[2], (4, 5))
         gather_and_interleave(1)
-        quantize(0)
+        quantize(0, (512, 128))
         for sums in multiply_chunk(0, 0, (0, 1)):
-            empty(nc.scalar.copy, *sums)
+            empty(*sums)
         gather_and_interleave(2)
-        quantize(1)
+        quantize(1, (1024,))
         for sums in multiply_chunk(0, 1, (6, 7)):
-            empty(nc.scalar.copy, *sums)
+            empty(*sums)
         held = multiply_chunk(1, 1, (2, 3)) + multiply_chunk(2, 1, (4, 5))
         gather_and_interleave(3)
         gather_and_interleave(4)
-        for c in (2, 3, 4):
-            quantize(c)
-        for s0, n, bank, copy in (
-            (chunk_at[2], 256, 0, nc.scalar.copy),
-            (chunk_at[2] + 256, 256, 1, nc.scalar.copy),
-            (chunk_at[3], 256, 6, nc.scalar.copy),
-            (chunk_at[4], 128, 7, nc.scalar.copy),
-        ):
-            empty(copy, *multiply(0, s0, n, bank))
+        quantize(2, (256, 256))
+        quantize(3, (256,))
+        quantize(4, (128,))
+        for s0, n, bank in ((1664, 256, 0), (1920, 256, 1), (2176, 256, 6), (2432, 128, 7)):
+            empty(*multiply(0, s0, n, bank))
         for sums in held:
-            empty(nc.scalar.copy, *sums)
+            empty(*sums)
         later = [cut for c in (4, 3, 0, 2) for cut in halves(chunk_at[c], CHUNKS[c])]
         for i, (j, (s0, n)) in enumerate([(j, cut) for cut in later for j in range(1, KT)]):
-            empty(nc.scalar.copy, *multiply(j, s0, n, 2 + i % 4))
+            empty(*multiply(j, s0, n, 2 + i % 4))
 
         def fetch(j, r, partial, t0, t1):
             total = keep.tile([P, t1 - t0], F32, name="sum%d_%d_%d" % (j, r, t0))
             window = dx[j][:].indirect(pos_sb[r][:, t0 // 16 : t1 // 16])
-            if r == 0:
+            if partial is None:
                 nc.vector.tensor_copy(total[:], window)
             else:
                 nc.vector.tensor_tensor(total[:], window, partial, ADD)
-            if r == TOP - 1:
-                nc.sync.dma_start(out[P * j : P * (j + 1), t0:t1], total[:])
             return total[:]
 
-        picked = [keep.tile([P, T], F32, name="picked%d" % r) for r in range(TOP)]
-        for r in range(TOP):
-            nc.vector.tensor_copy(picked[r][:], dx[0][:].indirect(pos_sb[r][:]))
-        turned = keep.tile([P, T], F32, name="turned")
-        result = keep.tile([P, T], F32, name="result")
-        for bank, (t0, n) in zip((2, 3), halves(0, T)):
-            acc = psum.tile([P, BANK], F32, name="bank%d" % bank)
-            for t in range(t0, t0 + n, P):
-                for r in range(TOP):
-                    nc.tensor.matmul(
-                        acc[:, t - t0 : t - t0 + P],
-                        picked[r][:, t : t + P],
-                        ident[:],
-                        start=(r == 0),
-                        stop=(r == TOP - 1),
-                        is_transpose=True,
-                    )
-            nc.scalar.copy(turned[:, t0 : t0 + n], acc[:, 0:n])
-        for bank, (t0, n) in zip((0, 1), halves(0, T)):
-            acc = psum.tile([P, BANK], F32, name="bank%d" % bank)
-            for t in range(t0, t0 + n, P):
-                nc.tensor.transpose(acc[:, t - t0 : t - t0 + P], turned[:, t : t + P], ident[:])
-            nc.scalar.copy(result[:, t0 : t0 + n], acc[:, 0:n])
-        nc.scalar.dma_start(out[0:P, :], result[:])
+        first_sum = fetch(0, 0, None, 0, T)
+        for r in range(1, TOP):
+            more = keep.tile([P, T], F32, name="first_sum%d" % r)
+            nc.gpsimd.tensor_tensor(more[:], first_sum, fetch(0, r, None, 0, T), ADD)
+            first_sum = more[:]
+        nc.scalar.dma_start(out[0:P, :], first_sum)
         second = third = None
         for r in range(TOP - 1):
             second = fetch(1, r, second, 0, T)
             third = fetch(2, r, third, 0, T)
-        fetch(1, TOP - 1, second, 0, T)
+        nc.sync.dma_start(out[P : 2 * P, :], fetch(1, TOP - 1, second, 0, T))
         for t0, n in zip(starts(LAST_CUTS), LAST_CUTS):
-            fetch(2, TOP - 1, third[:, t0 : t0 + n], t0, t0 + n)
+            nc.sync.dma_start(out[2 * P :, t0 : t0 + n], fetch(2, TOP - 1, third[:, t0 : t0 + n], t0, t0 + n))

@@ -25,23 +25,21 @@ P = 128
 PACK = 4
 KT = K // P
 BANK = 512
-CHUNKS = (640, 1024, 512, 256, 128)
+CHUNKS = (1280, 768, 384, 128)
 WINDOW = max(CHUNKS) + 16
-PLANES_AT = (0, 16384, 8192, 16384, 8192)
-HEAD_START = {1: 384, 2: 192}
+PLANES_AT = ((2304, 1280), (0, 768), (0, 1536), (384, 768))
+HEAD_START = {1: 384, 2: 128}
 LAST_CUTS = (352, 192, 96)
-BARE = 2
+EARLY = 8
+SPLIT = 1664
 
 
 def starts(widths):
     return [sum(widths[:i]) for i in range(len(widths))]
 
 
-def halves(s0, n):
-    if n <= BANK:
-        return [(s0, n)]
-    first = (n // C + 1) // 2 * C
-    return [(s0, first), (s0 + first, n - first)]
+def banks_of(s0, n):
+    return [(s, min(BANK, s0 + n - s)) for s in range(s0, s0 + n, BANK)]
 
 
 def tile_moe_bdx_lin_none_kernel(tc, dyT, w_words, w_scales, gate, offs, pos1, pos2, pos3, pos4, out):
@@ -56,14 +54,11 @@ def tile_moe_bdx_lin_none_kernel(tc, dyT, w_words, w_scales, gate, offs, pos1, p
         offs_sb = lists.tile([P, S // 16], U16, name="offs_sb")
         pos_sb = [lists.tile([P, T // 16], U16, name="pos_sb%d" % r) for r in range(TOP)]
         dy = [keep.tile([P, WINDOW], F32, name="dy%d" % t) for t in range(PACK)]
-        first_experts = [(chunk_at[c] // C, CHUNKS[c] // C) for c in range(2)]
-        w_first = [
-            keep.tile([P, ne, 2 * P], U8, name="w_first%d" % c, tag="w_first%d" % c, align_bytes=64)
-            for c, (e0, ne) in enumerate(first_experts)
-        ]
-        w_sb = keep.tile([P, E, 2 * K], U8, name="w_sb", align_bytes=64)
+        w_first = keep.tile([P, EARLY, 2 * P], U8, name="w_first", tag="w_first", align_bytes=64)
+        w_sb = keep.tile([P, E, 2 * (K - P)], U8, name="w_sb", align_bytes=64)
         ws_sb = keep.tile([P, E, K], U8, name="ws_sb", align_bytes=64)
-        dx = [keep.tile([P, S], F32, name="dx%d" % j) for j in range(KT)]
+        w_last = placed.tile([P, E - EARLY, 2 * P], U8, name="w_last", offset=4 * S - 1024, align_bytes=64)
+        dx = [keep.tile([P, S], F32, name="dx0")]
 
         gate_rows = keep.tile([P, P], F32, name="gate_rows")
         row0 = 32 - E
@@ -78,22 +73,16 @@ def tile_moe_bdx_lin_none_kernel(tc, dyT, w_words, w_scales, gate, offs, pos1, p
 
         dy_rows = dyT.rearrange("(p t) j -> p t j", t=PACK)
         nc.sync.dma_start(offs_sb[:], offs)
+        gate_sb = keep.tile([P, S], F32, name="gate_sb")
+        n0 = CHUNKS[0]
         for t in range(PACK):
             nc.sync.dma_start(dy[t][:, 0:T], dy_rows[:, t, :])
-        for (e0, ne), tile in zip(first_experts, w_first):
-            nc.sync.dma_start(
-                tile[:].bitcast(I32),
-                w_words[e0 : e0 + ne, 0, :, 0 : 2 * P].rearrange("e p b -> p e b").bitcast(I32),
-            )
-        early = sum(first_experts[-1])
-        nc.sync.dma_start(
-            w_sb[:, 0:early, 2 * P :].bitcast(I32),
-            w_words[0:early, 0, :, 2 * P :].rearrange("e p b -> p e b").bitcast(I32),
-        )
-        nc.sync.dma_start(
-            w_sb[:, early:, :].bitcast(I32),
-            w_words[early:, 0].rearrange("e p b -> p e b").bitcast(I32),
-        )
+            if t == 1:
+                nc.sync.dma_start(gate_sb[:, 0:n0], gate[0:P, 0:n0])
+        by_partition = w_words[:, 0].rearrange("e p b -> p e b")
+        nc.sync.dma_start(w_first[:].bitcast(I32), by_partition[:, 0:EARLY, 0 : 2 * P].bitcast(I32))
+        nc.sync.dma_start(w_last[:].bitcast(I32), by_partition[:, EARLY:, 0 : 2 * P].bitcast(I32))
+        nc.sync.dma_start(w_sb[:].bitcast(I32), by_partition[:, :, 2 * P :].bitcast(I32))
         for r in range(4):
             nc.sync.dma_start(
                 ws_sb[r:P:32].bitcast(I32),
@@ -113,87 +102,60 @@ def tile_moe_bdx_lin_none_kernel(tc, dyT, w_words, w_scales, gate, offs, pos1, p
 
         gate_col = keep.tile([P, E], F32, name="gate_col")
         nc.scalar.copy(gate_col[:], turn([gate_rows[:]], 0)[:, row0:32])
-        gate_sb = keep.tile([P, S], F32, name="gate_sb")
+        for bank, (s, m) in enumerate(banks_of(n0, S - n0)):
+            columns = [gate_col[:, e : e + 1].to_broadcast([P, P]) for e in range(s // C, (s + m) // C)]
+            nc.scalar.copy(gate_sb[:, s : s + m], turn(columns, 1 + bank)[:, 0:m])
 
-        def spread_gate(s0, n, banks):
-            for bank, (s, m) in zip(banks, halves(s0, n)):
-                columns = [gate_col[:, e : e + 1].to_broadcast([P, P]) for e in range(s // C, (s + m) // C)]
-                nc.scalar.copy(gate_sb[:, s : s + m], turn(columns, bank)[:, 0:m])
+        planes = keep.tile([P, PLANES_AT[0][0] + PACK * n0], F32, name="planes")
+        grouped = [keep.tile([P, SPLIT, PACK], BF16, name="grouped0", align_bytes=64)]
 
-        spread_gate(chunk_at[0], CHUNKS[0], (1, 2))
-        spread_gate(chunk_at[1], CHUNKS[1], (3, 0))
+        def grouped_at(s, m):
+            return grouped[0][:, s : s + m, :] if s < SPLIT else grouped[1][:, s - SPLIT : s - SPLIT + m, :]
 
-        grouped, g_codes, g_scales = {}, {}, {}
+        g_codes = keep.tile([P, S], U32, name="g_codes", align_bytes=64)
+        g_scales = keep.tile([P, S], U8, name="g_scales", align_bytes=64)
 
-        def gather_without_gate(t, plane):
-            n0 = CHUNKS[0]
-            bare = keep.tile([P, n0], F32, name="bare%d" % t)
-            nc.vector.tensor_copy(bare[:], dy[t][:].indirect(offs_sb[:, 0 : n0 // 16]))
-            gated = keep.tile([P, n0], F32, name="gated%d" % t)
-            for i, (s, m) in enumerate(halves(0, n0)):
-                acc = turn(blocks_of(bare, s, m), (1, 2, 3, 0)[2 * t + i])
-                for b in range(m // P):
-                    nc.scalar.activation(
-                        gated[:, s + P * b : s + P * (b + 1)],
-                        acc[:, P * b : P * (b + 1)],
-                        mybir.ActivationFunctionType.Copy,
-                        scale=gate_col[:, s // P + b : s // P + b + 1],
-                    )
-            for i, (s, m) in enumerate(halves(0, n0)):
-                nc.scalar.copy(plane[:, s : s + m], turn(blocks_of(gated, s, m), 4 + 2 * t + i)[:, 0:m])
+        def planes_of(c):
+            at, pitch = PLANES_AT[c]
+            return planes[:, at : at + PACK * pitch].rearrange("p (t s) -> p t s", t=PACK)
 
-        def gather_and_interleave(c):
-            s0, n = chunk_at[c], CHUNKS[c]
-            planes = placed.tile([P, PACK, n], F32, name="planes%d" % c, offset=PLANES_AT[c], align_bytes=64)
-            first = HEAD_START.get(c)
-            copies = [(s0, first), (s0 + first, n - first)] if first else halves(s0, n)
-            for t in range(PACK):
-                if c == 0 and t < BARE:
-                    gather_without_gate(t, planes[:, t, :])
-                    continue
-                for s, m in copies if first and t == PACK - 1 else [(s0, n)]:
-                    nc.vector.tensor_tensor(
-                        planes[:, t, s - s0 : s - s0 + m],
-                        dy[t][:].indirect(offs_sb[:, s // 16 : (s + m) // 16]),
-                        gate_sb[:, s : s + m],
-                        MULT,
-                    )
-            if c == 1:
-                grouped[c] = placed.tile([P, n, PACK], BF16, name="grouped1", offset=0, align_bytes=64)
-            else:
-                tag = "w_first%d" % (c - 2) if c in (2, 3) else "grouped%d" % c
-                grouped[c] = keep.tile([P, n, PACK], BF16, name="grouped%d" % c, tag=tag, align_bytes=64)
-            for s, m in copies:
-                nc.scalar.copy(
-                    grouped[c][:, s - s0 : s - s0 + m, :].rearrange("p (a i) t -> p a t i", i=4),
-                    planes[:, :, s - s0 : s - s0 + m].rearrange("p t (a i) -> p a t i", i=4),
-                )
+        def gather(c, t, s, m):
+            s0 = chunk_at[c] + s
+            nc.vector.tensor_tensor(
+                planes_of(c)[:, t, s : s + m],
+                dy[t][:].indirect(offs_sb[:, s0 // 16 : (s0 + m) // 16]),
+                gate_sb[:, s0 : s0 + m],
+                MULT,
+            )
 
-        def quantize(c, widths):
-            g_codes[c] = keep.tile([P, CHUNKS[c]], U32, name="codes%d" % c, align_bytes=64)
-            g_scales[c] = keep.tile([P, CHUNKS[c]], U8, name="scales%d" % c, align_bytes=64)
-            for s, m in zip(starts(widths), widths):
-                nc.vector.quantize_mx(
-                    out=g_codes[c][:, s : s + m].bitcast(FP8X4),
-                    scales=g_scales[c][:, s : s + m],
-                    in_=grouped[c][:, s : s + m, :].rearrange("p s t -> p (s t)"),
-                )
+        def interleave(c, s, m):
+            s0 = chunk_at[c] + s
+            nc.scalar.copy(
+                grouped_at(s0, m).rearrange("p (a i) t -> p a t i", i=4),
+                planes_of(c)[:, :, s : s + m].rearrange("p t (a i) -> p a t i", i=4),
+            )
+
+        def quantize(s, m):
+            nc.vector.quantize_mx(
+                out=g_codes[:, s : s + m].bitcast(FP8X4),
+                scales=g_scales[:, s : s + m],
+                in_=grouped_at(s, m).rearrange("p s t -> p (s t)"),
+            )
 
         def multiply(j, s0, n, bank):
             acc = psum.tile([P, BANK], F32, name="bank%d" % bank)
             for s in range(s0, s0 + n, C):
                 e = s // C
-                c = max(i for i in range(len(CHUNKS)) if chunk_at[i] <= s)
-                words = w_sb[:, e, 2 * P * j : 2 * P * (j + 1)]
-                if j == 0 and e < early:
-                    words = w_first[c][:, e - first_experts[c][0], :]
-                cols = slice(s - chunk_at[c], s - chunk_at[c] + C)
+                if j > 0:
+                    words = w_sb[:, e, 2 * P * (j - 1) : 2 * P * j]
+                else:
+                    words = w_first[:, e, :] if e < EARLY else w_last[:, e - EARLY, :]
                 nc.tensor.matmul_mx(
                     out=acc[:, s - s0 : s - s0 + C],
                     lhsT=words.bitcast(FP4X4),
-                    lhsT_scale=ws_sb[:, e, P * j : P * (j + 1)],
-                    rhs=g_codes[c][:, cols].bitcast(FP8X4),
-                    rhs_scale=g_scales[c][:, cols],
+                    lhsT_scale=ws_sb[:, s // C, P * j : P * (j + 1)],
+                    rhs=g_codes[:, s : s + C].bitcast(FP8X4),
+                    rhs_scale=g_scales[:, s : s + C],
                     start=True,
                     stop=True,
                 )
@@ -202,32 +164,63 @@ def tile_moe_bdx_lin_none_kernel(tc, dyT, w_words, w_scales, gate, offs, pos1, p
         def empty(j, s0, n, acc):
             nc.scalar.copy(dx[j][:, s0 : s0 + n], acc[:, 0:n])
 
-        def multiply_chunk(j, c, banks):
-            return [multiply(j, s, m, bank) for bank, (s, m) in zip(banks, halves(chunk_at[c], CHUNKS[c]))]
+        bare = keep.tile([P, n0], F32, name="bare")
+        nc.vector.tensor_copy(bare[:], dy[0][:].indirect(offs_sb[:, 0 : n0 // 16]))
+        gated = keep.tile([P, n0], F32, name="gated")
+        for i, (s, m) in enumerate(banks_of(0, n0)):
+            acc = turn(blocks_of(bare, s, m), 1 + i)
+            for b in range(m // P):
+                nc.scalar.activation(
+                    gated[:, s + P * b : s + P * (b + 1)],
+                    acc[:, P * b : P * (b + 1)],
+                    mybir.ActivationFunctionType.Copy,
+                    scale=gate_col[:, s // P + b : s // P + b + 1],
+                )
+        for i, (s, m) in enumerate(banks_of(0, n0)):
+            nc.scalar.copy(planes_of(0)[:, 0, s : s + m], turn(blocks_of(gated, s, m), 4 + i)[:, 0:m])
+        for t in range(1, PACK):
+            gather(0, t, 0, n0)
+        for s, m in ((0, 384), (384, 640), (1024, 256)):
+            interleave(0, s, m)
 
-        gather_and_interleave(0)
-        spread_gate(chunk_at[2], S - chunk_at[2], (4, 5))
-        gather_and_interleave(1)
-        quantize(0, (512, 128))
-        for sums in multiply_chunk(0, 0, (0, 1)):
-            empty(*sums)
-        gather_and_interleave(2)
-        quantize(1, (1024,))
-        for sums in multiply_chunk(0, 1, (6, 7)):
-            empty(*sums)
-        held = multiply_chunk(1, 1, (2, 3)) + multiply_chunk(2, 1, (4, 5))
-        gather_and_interleave(3)
-        gather_and_interleave(4)
-        quantize(2, (256, 256))
-        quantize(3, (256,))
-        quantize(4, (128,))
-        for s0, n, bank in ((1664, 256, 0), (1920, 256, 1), (2176, 256, 6), (2432, 128, 7)):
-            empty(*multiply(0, s0, n, bank))
+        for t in range(PACK - 1):
+            gather(1, t, 0, CHUNKS[1])
+        gather(1, PACK - 1, 0, 384)
+        quantize(0, 1024)
+        gather(1, PACK - 1, 384, 384)
+        first = [multiply(0, s, m, bank) for bank, (s, m) in enumerate(banks_of(0, 1024))]
+        interleave(1, 0, 384)
+        empty(*first[0])
+        grouped.append(keep.tile([P, S - SPLIT, PACK], BF16, name="grouped1", tag="w_first", align_bytes=64))
+        interleave(1, 384, 384)
+        empty(*first[1])
+
+        for t in (2, 3):
+            gather(2, t, 0, CHUNKS[2])
+        quantize(1024, 512)
+        quantize(1536, 128)
+        empty(*multiply(0, 1024, 512, 2))
+        empty(*multiply(0, 1536, 128, 3))
+        held = [multiply(1 + i % 2, BANK * (i // 2), BANK, 4 + i) for i in range(4)]
+        gather(2, 0, 0, CHUNKS[2])
+        for s, m in ((0, 128), (128, 256)):
+            gather(2, 1, s, m)
+            interleave(2, s, m)
+
+        for t in range(PACK):
+            gather(3, t, 0, CHUNKS[3])
+        interleave(3, 0, CHUNKS[3])
+        last = ((1664, 256), (1920, 256), (2176, 256), (2432, 128))
+        for s, m in last:
+            quantize(s, m)
+        for bank, (s, m) in enumerate(last):
+            empty(*multiply(0, s, m, bank))
+        for j in range(1, KT):
+            dx.append(placed.tile([P, S], F32, name="dx%d" % j, offset=4 * S * (j - 1), align_bytes=64))
         for sums in held:
             empty(*sums)
-        later = [cut for c in (4, 3, 0, 2) for cut in halves(chunk_at[c], CHUNKS[c])]
-        for i, (j, (s0, n)) in enumerate([(j, cut) for cut in later for j in range(1, KT)]):
-            empty(*multiply(j, s0, n, 2 + i % 4))
+        for i, (j, s0) in enumerate([(j, s0) for s0 in (1024, 1536, 2048) for j in range(1, KT)]):
+            empty(*multiply(j, s0, BANK, 4 + i % 4))
 
         def fetch(j, r, partial, t0, t1):
             total = keep.tile([P, t1 - t0], F32, name="sum%d_%d_%d" % (j, r, t0))

@@ -58,7 +58,7 @@ def tile_moe_bdx_lin_none_kernel(tc, dyT, w_words, w_scales, gate, offs, pos1, p
         w_sb = keep.tile([P, E, 2 * (K - P)], U8, name="w_sb", align_bytes=64)
         ws_sb = keep.tile([P, E, K], U8, name="ws_sb", align_bytes=64)
         w_last = placed.tile([P, E - EARLY, 2 * P], U8, name="w_last", offset=4 * S - 1024, align_bytes=64)
-        dx = [keep.tile([P, S], F32, name="dx0")]
+        dx = [keep.tile([P, S], F32, name="dx0", align_bytes=64)]
 
         gate_rows = keep.tile([P, P], F32, name="gate_rows")
         row0 = 32 - E
@@ -110,6 +110,8 @@ def tile_moe_bdx_lin_none_kernel(tc, dyT, w_words, w_scales, gate, offs, pos1, p
         grouped = [keep.tile([P, SPLIT, PACK], BF16, name="grouped0", align_bytes=64)]
 
         def grouped_at(s, m):
+            if s >= chunk_at[-1]:
+                return dx[0][:, SPLIT - 256 : SPLIT].bitcast(BF16).rearrange("p (s t) -> p s t", t=PACK)
             return grouped[0][:, s : s + m, :] if s < SPLIT else grouped[1][:, s - SPLIT : s - SPLIT + m, :]
 
         g_codes = keep.tile([P, S], U32, name="g_codes", align_bytes=64)
@@ -178,8 +180,10 @@ def tile_moe_bdx_lin_none_kernel(tc, dyT, w_words, w_scales, gate, offs, pos1, p
                 )
         for i, (s, m) in enumerate(banks_of(0, n0)):
             nc.scalar.copy(planes_of(0)[:, 0, s : s + m], turn(blocks_of(gated, s, m), 4 + i)[:, 0:m])
-        for t in range(1, PACK):
+        for t in range(1, PACK - 1):
             gather(0, t, 0, n0)
+        gather(0, PACK - 1, 0, 384)
+        gather(0, PACK - 1, 384, n0 - 384)
         for s, m in ((0, 384), (384, 640), (1024, 256)):
             interleave(0, s, m)
 
@@ -191,21 +195,21 @@ def tile_moe_bdx_lin_none_kernel(tc, dyT, w_words, w_scales, gate, offs, pos1, p
         first = [multiply(0, s, m, bank) for bank, (s, m) in enumerate(banks_of(0, 1024))]
         interleave(1, 0, 384)
         empty(*first[0])
-        grouped.append(keep.tile([P, S - SPLIT, PACK], BF16, name="grouped1", tag="w_first", align_bytes=64))
+        grouped.append(keep.tile([P, chunk_at[-1] - SPLIT, PACK], BF16, name="grouped1", tag="w_first", align_bytes=64))
         interleave(1, 384, 384)
         empty(*first[1])
 
         for t in (2, 3):
             gather(2, t, 0, CHUNKS[2])
         quantize(1024, 512)
-        quantize(1536, 128)
-        empty(*multiply(0, 1024, 512, 2))
-        empty(*multiply(0, 1536, 128, 3))
+        empty(*multiply(0, 1024, 384, 2))
         held = [multiply(1 + i % 2, BANK * (i // 2), BANK, 4 + i) for i in range(4)]
         gather(2, 0, 0, CHUNKS[2])
         for s, m in ((0, 128), (128, 256)):
             gather(2, 1, s, m)
             interleave(2, s, m)
+        quantize(1536, 128)
+        waiting = multiply(0, SPLIT - 256, 256, 3)[3]
 
         for t in range(PACK):
             gather(3, t, 0, CHUNKS[3])
@@ -213,7 +217,8 @@ def tile_moe_bdx_lin_none_kernel(tc, dyT, w_words, w_scales, gate, offs, pos1, p
         last = ((1664, 256), (1920, 256), (2176, 256), (2432, 128))
         for s, m in last:
             quantize(s, m)
-        for bank, (s, m) in enumerate(last):
+        nc.vector.tensor_copy(dx[0][:, SPLIT - 256 : SPLIT], waiting[:, 0:256])
+        for bank, (s, m) in zip((0, 1, 2, 0), last):
             empty(*multiply(0, s, m, bank))
         for j in range(1, KT):
             dx.append(placed.tile([P, S], F32, name="dx%d" % j, offset=4 * S * (j - 1), align_bytes=64))

@@ -30,6 +30,7 @@ WINDOW = max(CHUNKS) + 16
 PLANES_AT = ((2304, 1280), (0, 768), (0, 1536), (384, 768))
 HEAD_START = {1: 384, 2: 128}
 LAST_CUTS = (352, 192, 96)
+BARE = CHUNKS[0] + CHUNKS[1]
 EARLY = 8
 SPLIT = 1664
 
@@ -53,7 +54,7 @@ def tile_moe_bdx_lin_none_kernel(tc, dyT, w_words, w_scales, gate, offs, pos1, p
         chunk_at = starts(CHUNKS)
         offs_sb = lists.tile([P, S // 16], U16, name="offs_sb")
         pos_sb = [lists.tile([P, T // 16], U16, name="pos_sb%d" % r) for r in range(TOP)]
-        dy = [keep.tile([P, WINDOW], F32, name="dy%d" % t) for t in range(PACK)]
+        dy = [keep.tile([P, WINDOW if t else BARE + 16], F32, name="dy%d" % t) for t in range(PACK)]
         w_first = keep.tile([P, EARLY, 2 * P], U8, name="w_first", tag="w_first", align_bytes=64)
         w_sb = keep.tile([P, E, 2 * (K - P)], U8, name="w_sb", align_bytes=64)
         ws_sb = keep.tile([P, E, K], U8, name="ws_sb", align_bytes=64)
@@ -166,11 +167,11 @@ def tile_moe_bdx_lin_none_kernel(tc, dyT, w_words, w_scales, gate, offs, pos1, p
         def empty(j, s0, n, acc):
             nc.scalar.copy(dx[j][:, s0 : s0 + n], acc[:, 0:n])
 
-        bare = keep.tile([P, n0], F32, name="bare")
-        nc.vector.tensor_copy(bare[:], dy[0][:].indirect(offs_sb[:, 0 : n0 // 16]))
-        gated = keep.tile([P, n0], F32, name="gated")
-        for i, (s, m) in enumerate(banks_of(0, n0)):
-            acc = turn(blocks_of(bare, s, m), 1 + i)
+        bare = keep.tile([P, BARE], F32, name="bare")
+        nc.vector.tensor_copy(bare[:], dy[0][:].indirect(offs_sb[:, 0 : BARE // 16]))
+        gated = keep.tile([P, BARE], F32, name="gated")
+        for i, (s, m) in enumerate(banks_of(0, BARE)):
+            acc = turn(blocks_of(bare, s, m), (1, 2, 3, 0)[i])
             for b in range(m // P):
                 nc.scalar.activation(
                     gated[:, s + P * b : s + P * (b + 1)],
@@ -178,8 +179,10 @@ def tile_moe_bdx_lin_none_kernel(tc, dyT, w_words, w_scales, gate, offs, pos1, p
                     mybir.ActivationFunctionType.Copy,
                     scale=gate_col[:, s // P + b : s // P + b + 1],
                 )
-        for i, (s, m) in enumerate(banks_of(0, n0)):
-            nc.scalar.copy(planes_of(0)[:, 0, s : s + m], turn(blocks_of(gated, s, m), 4 + i)[:, 0:m])
+        back = [(c, s, m) for c in range(2) for s, m in banks_of(0, CHUNKS[c])]
+        for i, (c, s, m) in enumerate(back):
+            acc = turn(blocks_of(gated, chunk_at[c] + s, m), 4 + i % 4)
+            nc.scalar.copy(planes_of(c)[:, 0, s : s + m], acc[:, 0:m])
         for t in range(1, PACK - 1):
             gather(0, t, 0, n0)
         gather(0, PACK - 1, 0, 384)
@@ -187,7 +190,7 @@ def tile_moe_bdx_lin_none_kernel(tc, dyT, w_words, w_scales, gate, offs, pos1, p
         for s, m in ((0, 384), (384, 640), (1024, 256)):
             interleave(0, s, m)
 
-        for t in range(PACK - 1):
+        for t in range(1, PACK - 1):
             gather(1, t, 0, CHUNKS[1])
         gather(1, PACK - 1, 0, 384)
         quantize(0, 1024)

@@ -1,7 +1,6 @@
 from contextlib import ExitStack
 
 import concourse.mybir as mybir
-from concourse.masks import make_identity
 
 K, T, E, C, N = 384, 640, 20, 128, 512
 TOP = 4
@@ -20,27 +19,20 @@ FP8X4 = mybir.dt.float8_e4m3fn_x4
 FP4X4 = mybir.dt.float4_e2m1fn_x4
 MULT = mybir.AluOpType.mult
 ADD = mybir.AluOpType.add
+COPY = mybir.ActivationFunctionType.Copy
 
 P = 128
 PACK = 4
 KT = K // P
 BANK = 512
-CHUNKS = (1280, 768, 384, 128)
-WINDOW = max(CHUNKS) + 16
-PLANES_AT = ((2304, 1280), (0, 768), (0, 1536), (384, 768))
-HEAD_START = {1: 384, 2: 128}
+OWN = 640
+CHUNKS = (768, 640, 512)
+TOKEN_CUT = 256
 LAST_CUTS = (352, 192, 96)
-BARE = CHUNKS[0] + CHUNKS[1]
-EARLY = 8
-SPLIT = 1664
 
 
-def starts(widths):
-    return [sum(widths[:i]) for i in range(len(widths))]
-
-
-def banks_of(s0, n):
-    return [(s, min(BANK, s0 + n - s)) for s in range(s0, s0 + n, BANK)]
+def starts(widths, first=0):
+    return [first + sum(widths[:i]) for i in range(len(widths))]
 
 
 def tile_moe_bdx_lin_none_kernel(tc, dyT, w_words, w_scales, gate, offs, pos1, pos2, pos3, pos4, out):
@@ -48,115 +40,96 @@ def tile_moe_bdx_lin_none_kernel(tc, dyT, w_words, w_scales, gate, offs, pos1, p
     with ExitStack() as ctx:
         lists = ctx.enter_context(tc.tile_pool(name="lists", bufs=1))
         keep = ctx.enter_context(tc.tile_pool(name="keep", bufs=1))
-        placed = ctx.enter_context(tc.tile_pool(name="placed", bufs=1))
         psum = ctx.enter_context(tc.psum_pool(name="psum", bufs=1))
 
-        chunk_at = starts(CHUNKS)
+        a0, b0, c0 = starts(CHUNKS, OWN)
         offs_sb = lists.tile([P, S // 16], U16, name="offs_sb")
         pos_sb = [lists.tile([P, T // 16], U16, name="pos_sb%d" % r) for r in range(TOP)]
-        dy = [keep.tile([P, WINDOW if t else BARE + 16], F32, name="dy%d" % t) for t in range(PACK)]
-        w_first = keep.tile([P, EARLY, 2 * P], U8, name="w_first", tag="w_first", align_bytes=64)
-        w_sb = keep.tile([P, E, 2 * (K - P)], U8, name="w_sb", align_bytes=64)
+        dy = [keep.tile([P, max(CHUNKS) + 16], F32, name="dy%d" % t) for t in range(PACK)]
+        w_sb = keep.tile([P, E, 2 * K], U8, name="w_sb", align_bytes=64)
         ws_sb = keep.tile([P, E, K], U8, name="ws_sb", align_bytes=64)
-        w_last = placed.tile([P, E - EARLY, 2 * P], U8, name="w_last", offset=4 * S - 1024, align_bytes=64)
-        dx = [keep.tile([P, S], F32, name="dx0", align_bytes=64)]
+        gate_sb = keep.tile([P, S], F32, name="gate_sb")
+        na, nb, nc_ = CHUNKS
+        planes_a = keep.tile([P, PACK * na], F32, name="planes_a")
+        planes_b = keep.tile([P, PACK * nb], F32, name="planes_b")
+        planes_c = keep.tile([P, nc_ + PACK * OWN], F32, name="planes_c")
+        gate_own = planes_b[:, 2 * nb - OWN // 2 : 2 * nb + OWN // 2]
+        regions = (
+            (0, OWN, planes_c[:, nc_:]),
+            (a0, na, planes_a[:]),
+            (b0, nb, planes_b[:]),
+            (c0, nc_, planes_c[:, 0 : PACK * nc_]),
+        )
+        grouped = keep.tile([P, S, PACK], BF16, name="grouped", align_bytes=64)
+        g_codes = keep.tile([P, S], U32, name="g_codes", align_bytes=64)
+        g_scales = keep.tile([P, S], U8, name="g_scales", align_bytes=64)
+        dx = [keep.tile([P, S], F32, name="dx%d" % j) for j in range(KT)]
 
-        gate_rows = keep.tile([P, P], F32, name="gate_rows")
-        row0 = 32 - E
-        by_expert = gate[0].rearrange("(e c) -> e c", c=C)
-        nc.scalar.dma_start(gate_rows[row0 : row0 + 16, :], by_expert[0:16])
-        nc.scalar.dma_start(gate_rows[row0 + 16 : 32, :], by_expert[16:E])
-        for p0, p1 in ((0, row0), (32, 64), (64, P)):
-            nc.gpsimd.memset(gate_rows[p0:p1, :], 0.0)
-        ident = keep.tile([P, P], F32, name="ident")
-        make_identity(nc, ident[:])
         nc.vector.memset(ws_sb[:].bitcast(I32), 0)
 
         dy_rows = dyT.rearrange("(p t) j -> p t j", t=PACK)
         nc.sync.dma_start(offs_sb[:], offs)
-        gate_sb = keep.tile([P, S], F32, name="gate_sb")
-        n0 = CHUNKS[0]
         for t in range(PACK):
             nc.sync.dma_start(dy[t][:, 0:T], dy_rows[:, t, :])
-            if t == 1:
-                nc.sync.dma_start(gate_sb[:, 0:n0], gate[0:P, 0:n0])
+            if t == 0:
+                nc.sync.dma_start(gate_own, gate[0:P, 0:a0])
+        nc.sync.dma_start(gate_sb[:, a0:b0], gate[0:P, a0:b0])
+        nc.sync.dma_start(gate_sb[:, b0:S], gate[0:P, b0:S])
         by_partition = w_words[:, 0].rearrange("e p b -> p e b")
-        nc.sync.dma_start(w_first[:].bitcast(I32), by_partition[:, 0:EARLY, 0 : 2 * P].bitcast(I32))
-        nc.sync.dma_start(w_last[:].bitcast(I32), by_partition[:, EARLY:, 0 : 2 * P].bitcast(I32))
-        nc.sync.dma_start(w_sb[:].bitcast(I32), by_partition[:, :, 2 * P :].bitcast(I32))
+        for e0 in (0, E // 2):
+            nc.sync.dma_start(w_sb[:, e0 : e0 + E // 2].bitcast(I32), by_partition[:, e0 : e0 + E // 2].bitcast(I32))
+        for r, pos in enumerate((pos1, pos2, pos3, pos4)):
+            nc.sync.dma_start(pos_sb[r][:], pos)
         for r in range(4):
             nc.sync.dma_start(
                 ws_sb[r:P:32].bitcast(I32),
                 w_scales[:, 0, r:16:4, :].rearrange("e q k -> q e k").bitcast(I32),
             )
-        for r, pos in enumerate((pos1, pos2, pos3, pos4)):
-            nc.sync.dma_start(pos_sb[r][:], pos)
 
-        def turn(blocks, bank):
-            acc = psum.tile([P, BANK], F32, name="bank%d" % bank)
-            for i, block in enumerate(blocks):
-                nc.tensor.transpose(acc[:, P * i : P * (i + 1)], block, ident[:])
-            return acc
+        def region(s, m):
+            s0, n, rows = [r for r in regions if r[0] <= s < r[0] + r[1]][0]
+            return rows.rearrange("p (t s) -> p t s", t=PACK)[:, :, s - s0 : s - s0 + m]
 
-        def blocks_of(tile, s, m):
-            return [tile[:, b : b + P] for b in range(s, s + m, P)]
+        def plane(t, s, m):
+            return region(s, m)[:, t, :]
 
-        gate_col = keep.tile([P, E], F32, name="gate_col")
-        nc.scalar.copy(gate_col[:], turn([gate_rows[:]], 0)[:, row0:32])
-        for bank, (s, m) in enumerate(banks_of(n0, S - n0)):
-            columns = [gate_col[:, e : e + 1].to_broadcast([P, P]) for e in range(s // C, (s + m) // C)]
-            nc.scalar.copy(gate_sb[:, s : s + m], turn(columns, 1 + bank)[:, 0:m])
+        def window(t, s, m):
+            return dy[t][:].indirect(offs_sb[:, s // 16 : (s + m) // 16])
 
-        planes = keep.tile([P, PLANES_AT[0][0] + PACK * n0], F32, name="planes")
-        grouped = [keep.tile([P, SPLIT, PACK], BF16, name="grouped0", align_bytes=64)]
+        def gather_bare(t, s, m):
+            nc.scalar.activation(plane(t, s, m), window(t, s, m), COPY)
 
-        def grouped_at(s, m):
-            if s >= chunk_at[-1]:
-                return dx[0][:, SPLIT - 256 : SPLIT].bitcast(BF16).rearrange("p (s t) -> p s t", t=PACK)
-            return grouped[0][:, s : s + m, :] if s < SPLIT else grouped[1][:, s - SPLIT : s - SPLIT + m, :]
+        def gather_gated(t, s, m):
+            nc.vector.tensor_tensor(plane(t, s, m), window(t, s, m), gate_own[:, s : s + m], MULT)
 
-        g_codes = keep.tile([P, S], U32, name="g_codes", align_bytes=64)
-        g_scales = keep.tile([P, S], U8, name="g_scales", align_bytes=64)
+        def woven(s, m):
+            return grouped[:, s : s + m, :].rearrange("p (a i) t -> p a t i", i=4)
 
-        def planes_of(c):
-            at, pitch = PLANES_AT[c]
-            return planes[:, at : at + PACK * pitch].rearrange("p (t s) -> p t s", t=PACK)
+        def four_planes(s, m):
+            return region(s, m).rearrange("p t (a i) -> p a t i", i=4)
 
-        def gather(c, t, s, m):
-            s0 = chunk_at[c] + s
-            nc.vector.tensor_tensor(
-                planes_of(c)[:, t, s : s + m],
-                dy[t][:].indirect(offs_sb[:, s0 // 16 : (s0 + m) // 16]),
-                gate_sb[:, s0 : s0 + m],
-                MULT,
-            )
+        def weave(s, m):
+            nc.vector.tensor_copy(woven(s, m), four_planes(s, m))
 
-        def interleave(c, s, m):
-            s0 = chunk_at[c] + s
-            nc.scalar.copy(
-                grouped_at(s0, m).rearrange("p (a i) t -> p a t i", i=4),
-                planes_of(c)[:, :, s : s + m].rearrange("p t (a i) -> p a t i", i=4),
-            )
+        def gate_and_weave(s, m):
+            spread = gate_sb[:, s : s + m].rearrange("p (a i) -> p a i", i=4).unsqueeze(2).to_broadcast([P, m // 4, PACK, 4])
+            nc.vector.tensor_tensor(woven(s, m), four_planes(s, m), spread, MULT)
 
         def quantize(s, m):
             nc.vector.quantize_mx(
                 out=g_codes[:, s : s + m].bitcast(FP8X4),
                 scales=g_scales[:, s : s + m],
-                in_=grouped_at(s, m).rearrange("p s t -> p (s t)"),
+                in_=grouped[:, s : s + m, :].rearrange("p s t -> p (s t)"),
             )
 
         def multiply(j, s0, n, bank):
             acc = psum.tile([P, BANK], F32, name="bank%d" % bank)
             for s in range(s0, s0 + n, C):
                 e = s // C
-                if j > 0:
-                    words = w_sb[:, e, 2 * P * (j - 1) : 2 * P * j]
-                else:
-                    words = w_first[:, e, :] if e < EARLY else w_last[:, e - EARLY, :]
                 nc.tensor.matmul_mx(
                     out=acc[:, s - s0 : s - s0 + C],
-                    lhsT=words.bitcast(FP4X4),
-                    lhsT_scale=ws_sb[:, s // C, P * j : P * (j + 1)],
+                    lhsT=w_sb[:, e, 2 * P * j : 2 * P * (j + 1)].bitcast(FP4X4),
+                    lhsT_scale=ws_sb[:, e, P * j : P * (j + 1)],
                     rhs=g_codes[:, s : s + C].bitcast(FP8X4),
                     rhs_scale=g_scales[:, s : s + C],
                     start=True,
@@ -167,88 +140,75 @@ def tile_moe_bdx_lin_none_kernel(tc, dyT, w_words, w_scales, gate, offs, pos1, p
         def empty(j, s0, n, acc):
             nc.scalar.copy(dx[j][:, s0 : s0 + n], acc[:, 0:n])
 
-        bare = keep.tile([P, BARE], F32, name="bare")
-        nc.vector.tensor_copy(bare[:], dy[0][:].indirect(offs_sb[:, 0 : BARE // 16]))
-        gated = keep.tile([P, BARE], F32, name="gated")
-        for i, (s, m) in enumerate(banks_of(0, BARE)):
-            acc = turn(blocks_of(bare, s, m), (1, 2, 3, 0)[i])
-            for b in range(m // P):
-                nc.scalar.activation(
-                    gated[:, s + P * b : s + P * (b + 1)],
-                    acc[:, P * b : P * (b + 1)],
-                    mybir.ActivationFunctionType.Copy,
-                    scale=gate_col[:, s // P + b : s // P + b + 1],
-                )
-        back = [(c, s, m) for c in range(2) for s, m in banks_of(0, CHUNKS[c])]
-        for i, (c, s, m) in enumerate(back):
-            acc = turn(blocks_of(gated, chunk_at[c] + s, m), 4 + i % 4)
-            nc.scalar.copy(planes_of(c)[:, 0, s : s + m], acc[:, 0:m])
-        for t in range(1, PACK - 1):
-            gather(0, t, 0, n0)
-        gather(0, PACK - 1, 0, 384)
-        gather(0, PACK - 1, 384, n0 - 384)
-        for s, m in ((0, 384), (384, 640), (1024, 256)):
-            interleave(0, s, m)
+        def empty_on_vector(j, s0, n, acc):
+            nc.vector.tensor_copy(dx[j][:, s0 : s0 + n], acc[:, 0:n])
 
-        for t in range(1, PACK - 1):
-            gather(1, t, 0, CHUNKS[1])
-        gather(1, PACK - 1, 0, 384)
-        quantize(0, 1024)
-        gather(1, PACK - 1, 384, 384)
-        first = [multiply(0, s, m, bank) for bank, (s, m) in enumerate(banks_of(0, 1024))]
-        interleave(1, 0, 384)
-        empty(*first[0])
-        grouped.append(keep.tile([P, chunk_at[-1] - SPLIT, PACK], BF16, name="grouped1", tag="w_first", align_bytes=64))
-        interleave(1, 384, 384)
-        empty(*first[1])
+        gather_bare(0, a0, na)
+        gather_bare(0, b0, nb)
+        nc.vector.tensor_copy(plane(0, c0, S - c0), window(0, c0, S - c0))
+        for t in range(1, PACK):
+            gather_bare(t, a0, na)
+        for t in range(PACK - 1):
+            gather_gated(t, 0, OWN)
+        for s, m in ((0, 384), (384, 256)):
+            gather_gated(PACK - 1, s, m)
+        for s, m in ((0, 384), (384, 256)):
+            weave(s, m)
+        quantize(0, 384)
+        for s0, n in ((b0, nb), (c0, nc_)):
+            for t in range(1, PACK):
+                gather_bare(t, s0, n)
+        pieces = ((384, 256), (a0, 384), (a0 + 384, 384), (b0, 384), (b0 + 384, 256), (c0, 384), (c0 + 384, 128))
+        for before, piece in zip(pieces, pieces[1:]):
+            gate_and_weave(*piece)
+            quantize(*before)
+        quantize(*pieces[-1])
 
-        for t in (2, 3):
-            gather(2, t, 0, CHUNKS[2])
-        quantize(1024, 512)
-        empty(*multiply(0, 1024, 384, 2))
-        held = [multiply(1 + i % 2, BANK * (i // 2), BANK, 4 + i) for i in range(4)]
-        gather(2, 0, 0, CHUNKS[2])
-        for s, m in ((0, 128), (128, 256)):
-            gather(2, 1, s, m)
-            interleave(2, s, m)
-        quantize(1536, 128)
-        waiting = multiply(0, SPLIT - 256, 256, 3)[3]
-
-        for t in range(PACK):
-            gather(3, t, 0, CHUNKS[3])
-        interleave(3, 0, CHUNKS[3])
-        last = ((1664, 256), (1920, 256), (2176, 256), (2432, 128))
-        for s, m in last:
-            quantize(s, m)
-        nc.vector.tensor_copy(dx[0][:, SPLIT - 256 : SPLIT], waiting[:, 0:256])
-        for bank, (s, m) in zip((0, 1, 2, 0), last):
-            empty(*multiply(0, s, m, bank))
-        for j in range(1, KT):
-            dx.append(placed.tile([P, S], F32, name="dx%d" % j, offset=4 * S * (j - 1), align_bytes=64))
-        for sums in held:
+        first = [multiply(0, s, m, bank) for bank, (s, m) in enumerate(((0, 512), (512, 512), (1024, 384)))]
+        held = [multiply(1, BANK * i, BANK, 6 + i) for i in range(2)]
+        first.append(multiply(0, 1408, 512, 3))
+        for sums in first[:3]:
             empty(*sums)
-        for i, (j, s0) in enumerate([(j, s0) for s0 in (1024, 1536, 2048) for j in range(1, KT)]):
-            empty(*multiply(j, s0, BANK, 4 + i % 4))
+        held += [multiply(1, BANK * (2 + i), BANK, i) for i in range(2)]
+        empty(*first[3])
+        empty(*held[0])
+        empty(*multiply(0, 1920, 512, 4))
+        empty(*multiply(0, 2432, 128, 5))
+        held.append(multiply(1, 2048, BANK, 2))
+        for sums in held[1:3]:
+            empty_on_vector(*sums)
 
         def fetch(j, r, partial, t0, t1):
             total = keep.tile([P, t1 - t0], F32, name="sum%d_%d_%d" % (j, r, t0))
-            window = dx[j][:].indirect(pos_sb[r][:, t0 // 16 : t1 // 16])
-            if partial is None:
-                nc.vector.tensor_copy(total[:], window)
-            else:
-                nc.vector.tensor_tensor(total[:], window, partial, ADD)
+            nc.vector.tensor_tensor(total[:], dx[j][:].indirect(pos_sb[r][:, t0 // 16 : t1 // 16]), partial, ADD)
             return total[:]
 
-        first_sum = fetch(0, 0, None, 0, T)
-        for r in range(1, TOP):
-            more = keep.tile([P, T], F32, name="first_sum%d" % r)
-            nc.gpsimd.tensor_tensor(more[:], first_sum, fetch(0, r, None, 0, T), ADD)
-            first_sum = more[:]
-        nc.scalar.dma_start(out[0:P, :], first_sum)
-        second = third = None
-        for r in range(TOP - 1):
-            second = fetch(1, r, second, 0, T)
-            third = fetch(2, r, third, 0, T)
-        nc.sync.dma_start(out[P : 2 * P, :], fetch(1, TOP - 1, second, 0, T))
-        for t0, n in zip(starts(LAST_CUTS), LAST_CUTS):
-            nc.sync.dma_start(out[2 * P :, t0 : t0 + n], fetch(2, TOP - 1, third[:, t0 : t0 + n], t0, t0 + n))
+        def fetch_bare(j, r, t0, t1):
+            got = keep.tile([P, t1 - t0], F32, name="got%d_%d_%d" % (j, r, t0))
+            nc.scalar.activation(got[:], dx[j][:].indirect(pos_sb[r][:, t0 // 16 : t1 // 16]), COPY)
+            return got[:]
+
+        halves = ((0, TOKEN_CUT), (TOKEN_CUT, T))
+
+        def chain(j, heads):
+            for r in range(1, TOP):
+                heads = [fetch(j, r, head, *half) for head, half in zip(heads, halves)]
+            for head, (t0, t1) in zip(heads, halves):
+                nc.sync.dma_start(out[P * j : P * (j + 1), t0:t1], head)
+
+        heads0 = [fetch_bare(0, 0, *half) for half in halves]
+        for sums in held[3:]:
+            empty(*sums)
+        head1 = fetch_bare(1, 0, 0, T)
+        for i, bank in enumerate((3, 4, 5, 6, 7)):
+            empty(*multiply(2, BANK * i, BANK, bank))
+        parts = [fetch_bare(2, r, 0, T) for r in range(TOP - 1)]
+        chain(0, heads0)
+        chain(1, [head1[:, t0:t1] for t0, t1 in halves])
+        sums = [fetch(2, TOP - 1, parts[0][:, t0:t1], t0, t1) for t0, t1 in halves]
+        pair = keep.tile([P, T], F32, name="pair")
+        nc.vector.tensor_tensor(pair[:], parts[1], parts[2], ADD)
+        total = keep.tile([P, T], F32, name="total")
+        for part, (t0, t1) in zip(sums, halves):
+            nc.vector.tensor_tensor(total[:, t0:t1], part, pair[:, t0:t1], ADD)
+            nc.sync.dma_start(out[2 * P :, t0:t1], total[:, t0:t1])

@@ -28,7 +28,7 @@ BANK = 512
 OWN = 640
 CHUNKS = (768, 640, 512)
 TOKEN_CUT = 256
-LAST_CUTS = (352, 192, 96)
+LAST_CUTS = ((0, 384), (384, 640))
 
 
 def starts(widths, first=0):
@@ -40,6 +40,7 @@ def tile_moe_bdx_lin_none_kernel(tc, dyT, w_words, w_scales, gate, offs, pos1, p
     with ExitStack() as ctx:
         lists = ctx.enter_context(tc.tile_pool(name="lists", bufs=1))
         keep = ctx.enter_context(tc.tile_pool(name="keep", bufs=1))
+        placed = ctx.enter_context(tc.tile_pool(name="placed", bufs=1))
         psum = ctx.enter_context(tc.psum_pool(name="psum", bufs=1))
 
         a0, b0, c0 = starts(CHUNKS, OWN)
@@ -63,9 +64,10 @@ def tile_moe_bdx_lin_none_kernel(tc, dyT, w_words, w_scales, gate, offs, pos1, p
         grouped = keep.tile([P, S, PACK], BF16, name="grouped", align_bytes=64)
         g_codes = keep.tile([P, S], U32, name="g_codes", align_bytes=64)
         g_scales = keep.tile([P, S], U8, name="g_scales", align_bytes=64)
-        dx = [keep.tile([P, S], F32, name="dx%d" % j) for j in range(KT)]
+        dx = [keep.tile([P, S], F32, name="dx%d" % j) for j in range(KT - 1)]
 
-        nc.vector.memset(ws_sb[:].bitcast(I32), 0)
+        nc.vector.memset(ws_sb[:, 0 : E // 2].bitcast(I32), 0)
+        nc.scalar.copy(ws_sb[:, E // 2 :].bitcast(U32), ws_sb[:, 0 : E // 2].bitcast(U32))
 
         dy_rows = dyT.rearrange("(p t) j -> p t j", t=PACK)
         nc.sync.dma_start(offs_sb[:], offs)
@@ -164,51 +166,59 @@ def tile_moe_bdx_lin_none_kernel(tc, dyT, w_words, w_scales, gate, offs, pos1, p
             quantize(*before)
         quantize(*pieces[-1])
 
-        first = [multiply(0, s, m, bank) for bank, (s, m) in enumerate(((0, 512), (512, 512), (1024, 384)))]
+        first = [multiply(0, s, m, bank) for bank, (s, m) in enumerate(((0, 512), (512, 512), (1024, 512), (1536, 256)))]
         held = [multiply(1, BANK * i, BANK, 6 + i) for i in range(2)]
-        first.append(multiply(0, 1408, 512, 3))
-        for sums in first[:3]:
+        for sums in first + held:
             empty(*sums)
-        held += [multiply(1, BANK * (2 + i), BANK, i) for i in range(2)]
-        empty(*first[3])
-        empty(*held[0])
-        empty(*multiply(0, 1920, 512, 4))
-        empty(*multiply(0, 2432, 128, 5))
-        held.append(multiply(1, 2048, BANK, 2))
-        for sums in held[1:3]:
-            empty_on_vector(*sums)
+        held = [multiply(1, 1024, BANK, 0)]
+        empty(*multiply(0, 1792, 256, 4))
+        held.append(multiply(1, 1536, BANK, 1))
+        for sums in held:
+            empty(*sums)
+        empty_on_vector(*multiply(0, 2048, 384, 5))
+        empty_on_vector(*multiply(0, 2432, 128, 3))
+        empty_on_vector(*multiply(1, 2048, BANK, 2))
 
-        def fetch(j, r, partial, t0, t1):
-            total = keep.tile([P, t1 - t0], F32, name="sum%d_%d_%d" % (j, r, t0))
-            nc.vector.tensor_tensor(total[:], dx[j][:].indirect(pos_sb[r][:, t0 // 16 : t1 // 16]), partial, ADD)
-            return total[:]
+        def listed(j, r, t0, t1):
+            return dx[j][:].indirect(pos_sb[r][:, t0 // 16 : t1 // 16])
 
-        def fetch_bare(j, r, t0, t1):
-            got = keep.tile([P, t1 - t0], F32, name="got%d_%d_%d" % (j, r, t0))
-            nc.scalar.activation(got[:], dx[j][:].indirect(pos_sb[r][:, t0 // 16 : t1 // 16]), COPY)
-            return got[:]
+        def fetch_bare(j, r, got, cuts):
+            for t0, t1 in cuts:
+                nc.scalar.activation(got[:, t0:t1], listed(j, r, t0, t1), COPY)
+            return got
+
+        def fetch(j, r, total, partial, cuts):
+            for t0, t1 in cuts:
+                nc.vector.tensor_tensor(total[:, t0:t1], listed(j, r, t0, t1), partial[:, t0:t1], ADD)
+            return total
+
+        def fresh(name):
+            return keep.tile([P, T], F32, name=name)[:]
 
         halves = ((0, TOKEN_CUT), (TOKEN_CUT, T))
-
-        def chain(j, heads):
-            for r in range(1, TOP):
-                heads = [fetch(j, r, head, *half) for head, half in zip(heads, halves)]
-            for head, (t0, t1) in zip(heads, halves):
-                nc.sync.dma_start(out[P * j : P * (j + 1), t0:t1], head)
-
-        heads0 = [fetch_bare(0, 0, *half) for half in halves]
-        for sums in held[3:]:
-            empty(*sums)
-        head1 = fetch_bare(1, 0, 0, T)
-        for i, bank in enumerate((3, 4, 5, 6, 7)):
+        whole = ((0, T),)
+        head0 = placed.tile([P, T], F32, name="head0", offset=0)
+        shared = keep.tile([P, 2 * T - TOKEN_CUT], F32, name="shared")
+        sum0 = fetch_bare(0, 0, head0[:], halves)
+        heads1 = [fetch_bare(1, r, fresh("head1_%d" % r), whole) for r in range(2)]
+        sum0 = fetch(0, 1, shared[:, T - TOKEN_CUT :], sum0, halves)
+        dx.append(placed.tile([P, S], F32, name="dx2", offset=0))
+        for i, bank in enumerate((6, 7, 0, 4, 1)):
             empty(*multiply(2, BANK * i, BANK, bank))
-        parts = [fetch_bare(2, r, 0, T) for r in range(TOP - 1)]
-        chain(0, heads0)
-        chain(1, [head1[:, t0:t1] for t0, t1 in halves])
-        sums = [fetch(2, TOP - 1, parts[0][:, t0:t1], t0, t1) for t0, t1 in halves]
-        pair = keep.tile([P, T], F32, name="pair")
-        nc.vector.tensor_tensor(pair[:], parts[1], parts[2], ADD)
-        total = keep.tile([P, T], F32, name="total")
-        for part, (t0, t1) in zip(sums, halves):
-            nc.vector.tensor_tensor(total[:, t0:t1], part, pair[:, t0:t1], ADD)
+        heads2 = [fetch_bare(2, r, fresh("head2_%d" % r), LAST_CUTS if r == 2 else whole) for r in range(TOP - 1)]
+        sum0 = fetch(0, 2, fresh("sum0_2"), sum0, halves)
+        low1 = fetch(1, 2, shared[:, 0:T], heads1[0], whole)
+        sum0 = fetch(0, 3, fresh("sum0_3"), sum0, whole)
+        nc.sync.dma_start(out[0:P, :], sum0)
+        high1 = fetch(1, 3, fresh("high1"), heads1[1], whole)
+        sum2 = fetch(2, 3, fresh("sum2_3"), heads2[0], whole)
+        sum1 = fresh("sum1")
+        nc.vector.tensor_tensor(sum1, low1, high1, ADD)
+        nc.sync.dma_start(out[P : 2 * P, :], sum1)
+        more2 = fresh("more2")
+        for t0, t1 in LAST_CUTS:
+            nc.vector.tensor_tensor(more2[:, t0:t1], sum2[:, t0:t1], heads2[1][:, t0:t1], ADD)
+        total = fresh("total")
+        for t0, t1 in LAST_CUTS:
+            nc.vector.tensor_tensor(total[:, t0:t1], more2[:, t0:t1], heads2[2][:, t0:t1], ADD)
             nc.sync.dma_start(out[2 * P :, t0:t1], total[:, t0:t1])

@@ -1,6 +1,7 @@
 from contextlib import ExitStack
 
 import concourse.mybir as mybir
+from concourse.masks import make_identity
 
 K, T, E, C, N = 384, 640, 20, 128, 512
 TOP = 4
@@ -25,10 +26,11 @@ P = 128
 PACK = 4
 KT = K // P
 BANK = 512
-OWN = 640
-CHUNKS = (768, 640, 512)
+OWN = 768
+CHUNKS = (1024, 512, 256)
 TOKEN_CUT = 256
 LAST_CUTS = ((0, 384), (384, 640))
+HELPED = 256
 
 
 def starts(widths, first=0):
@@ -46,28 +48,32 @@ def tile_moe_bdx_lin_none_kernel(tc, dyT, w_words, w_scales, gate, offs, pos1, p
         a0, b0, c0 = starts(CHUNKS, OWN)
         offs_sb = lists.tile([P, S // 16], U16, name="offs_sb")
         pos_sb = [lists.tile([P, T // 16], U16, name="pos_sb%d" % r) for r in range(TOP)]
-        dy = [keep.tile([P, max(CHUNKS) + 16], F32, name="dy%d" % t) for t in range(PACK)]
+        dy = [keep.tile([P, max(CHUNKS) + 16], F32, name="dy%d" % t) for t in range(PACK - 1)]
+        dy.append(placed.tile([P, max(CHUNKS) + 16], F32, name="dy3", offset=8 * S - 2048))
         w_sb = keep.tile([P, E, 2 * K], U8, name="w_sb", align_bytes=64)
         ws_sb = keep.tile([P, E, K], U8, name="ws_sb", align_bytes=64)
         gate_sb = keep.tile([P, S], F32, name="gate_sb")
         na, nb, nc_ = CHUNKS
-        planes_a = keep.tile([P, PACK * na], F32, name="planes_a")
-        planes_b = keep.tile([P, PACK * nb], F32, name="planes_b")
-        planes_c = keep.tile([P, nc_ + PACK * OWN], F32, name="planes_c")
-        gate_own = planes_b[:, 2 * nb - OWN // 2 : 2 * nb + OWN // 2]
+        pitch_b = PACK * na + nc_
+        at_a = 2 * pitch_b
+        planes = keep.tile([P, PACK * pitch_b], F32, name="planes")
+        planes_own = keep.tile([P, PACK * OWN], F32, name="planes_own")
+        gate_own = planes[:, pitch_b : pitch_b + OWN]
         regions = (
-            (0, OWN, planes_c[:, nc_:]),
-            (a0, na, planes_a[:]),
-            (b0, nb, planes_b[:]),
-            (c0, nc_, planes_c[:, 0 : PACK * nc_]),
+            (0, planes_own[:]),
+            (a0, planes[:, at_a : at_a + PACK * na]),
+            (b0, planes[:]),
+            (c0, planes[:, at_a + na : at_a + (PACK + 1) * na]),
         )
         grouped = keep.tile([P, S, PACK], BF16, name="grouped", align_bytes=64)
         g_codes = keep.tile([P, S], U32, name="g_codes", align_bytes=64)
         g_scales = keep.tile([P, S], U8, name="g_scales", align_bytes=64)
-        dx = [keep.tile([P, S], F32, name="dx%d" % j) for j in range(KT - 1)]
 
-        nc.vector.memset(ws_sb[:, 0 : E // 2].bitcast(I32), 0)
-        nc.scalar.copy(ws_sb[:, E // 2 :].bitcast(U32), ws_sb[:, 0 : E // 2].bitcast(U32))
+        nc.vector.memset(ws_sb[:, 0:2].bitcast(I32), 0)
+        nc.scalar.copy(ws_sb[:, 2:4].bitcast(U32), ws_sb[:, 0:2].bitcast(U32))
+        nc.vector.memset(ws_sb[:, 4:].bitcast(I32), 0)
+        ident = keep.tile([P, P], F32, name="ident")
+        make_identity(nc, ident[:])
 
         dy_rows = dyT.rearrange("(p t) j -> p t j", t=PACK)
         nc.sync.dma_start(offs_sb[:], offs)
@@ -75,7 +81,9 @@ def tile_moe_bdx_lin_none_kernel(tc, dyT, w_words, w_scales, gate, offs, pos1, p
             nc.sync.dma_start(dy[t][:, 0:T], dy_rows[:, t, :])
             if t == 0:
                 nc.sync.dma_start(gate_own, gate[0:P, 0:a0])
-        nc.sync.dma_start(gate_sb[:, a0:b0], gate[0:P, a0:b0])
+        gate_col = keep.tile([P, na // C], F32, name="gate_col")
+        with nc.allow_non_contiguous_dma(reason="one gate a partition"):
+            nc.sync.dma_start(gate_col[:], gate[0, a0:b0].rearrange("(e c) -> c e", c=C))
         nc.sync.dma_start(gate_sb[:, b0:S], gate[0:P, b0:S])
         by_partition = w_words[:, 0].rearrange("e p b -> p e b")
         for e0 in (0, E // 2):
@@ -89,7 +97,7 @@ def tile_moe_bdx_lin_none_kernel(tc, dyT, w_words, w_scales, gate, offs, pos1, p
             )
 
         def region(s, m):
-            s0, n, rows = [r for r in regions if r[0] <= s < r[0] + r[1]][0]
+            s0, rows = [r for r in regions if r[0] <= s][-1]
             return rows.rearrange("p (t s) -> p t s", t=PACK)[:, :, s - s0 : s - s0 + m]
 
         def plane(t, s, m):
@@ -111,10 +119,10 @@ def tile_moe_bdx_lin_none_kernel(tc, dyT, w_words, w_scales, gate, offs, pos1, p
             return region(s, m).rearrange("p t (a i) -> p a t i", i=4)
 
         def weave(s, m):
-            nc.vector.tensor_copy(woven(s, m), four_planes(s, m))
+            nc.gpsimd.tensor_scalar(woven(s, m), four_planes(s, m), 1.0, 0.0, MULT, ADD)
 
-        def gate_and_weave(s, m):
-            spread = gate_sb[:, s : s + m].rearrange("p (a i) -> p a i", i=4).unsqueeze(2).to_broadcast([P, m // 4, PACK, 4])
+        def gate_and_weave(s, m, gates):
+            spread = gates.rearrange("p (a i) -> p a i", i=4).unsqueeze(2).to_broadcast([P, m // 4, PACK, 4])
             nc.vector.tensor_tensor(woven(s, m), four_planes(s, m), spread, MULT)
 
         def quantize(s, m):
@@ -145,39 +153,46 @@ def tile_moe_bdx_lin_none_kernel(tc, dyT, w_words, w_scales, gate, offs, pos1, p
         def empty_on_vector(j, s0, n, acc):
             nc.vector.tensor_copy(dx[j][:, s0 : s0 + n], acc[:, 0:n])
 
-        gather_bare(0, a0, na)
-        gather_bare(0, b0, nb)
-        nc.vector.tensor_copy(plane(0, c0, S - c0), window(0, c0, S - c0))
-        for t in range(1, PACK):
-            gather_bare(t, a0, na)
-        for t in range(PACK - 1):
-            gather_gated(t, 0, OWN)
-        for s, m in ((0, 384), (384, 256)):
-            gather_gated(PACK - 1, s, m)
-        for s, m in ((0, 384), (384, 256)):
-            weave(s, m)
-        quantize(0, 384)
-        for s0, n in ((b0, nb), (c0, nc_)):
-            for t in range(1, PACK):
-                gather_bare(t, s0, n)
-        pieces = ((384, 256), (a0, 384), (a0 + 384, 384), (b0, 384), (b0 + 384, 256), (c0, 384), (c0 + 384, 128))
-        for before, piece in zip(pieces, pieces[1:]):
-            gate_and_weave(*piece)
-            quantize(*before)
-        quantize(*pieces[-1])
+        def gate_in_psum(s, m, bank):
+            acc = psum.tile([P, BANK], F32, name="bank%d" % bank)
+            for i in range(m // C):
+                e = (s - a0) // C + i
+                nc.tensor.transpose(acc[:, C * i : C * (i + 1)], gate_col[:, e : e + 1].to_broadcast([P, P]), ident[:])
+            return acc[:, 0:m]
 
-        first = [multiply(0, s, m, bank) for bank, (s, m) in enumerate(((0, 512), (512, 512), (1024, 512), (1536, 256)))]
-        held = [multiply(1, BANK * i, BANK, 6 + i) for i in range(2)]
-        for sums in first + held:
-            empty(*sums)
-        held = [multiply(1, 1024, BANK, 0)]
-        empty(*multiply(0, 1792, 256, 4))
-        held.append(multiply(1, 1536, BANK, 1))
-        for sums in held:
-            empty(*sums)
-        empty_on_vector(*multiply(0, 2048, 384, 5))
-        empty_on_vector(*multiply(0, 2432, 128, 3))
-        empty_on_vector(*multiply(1, 2048, BANK, 2))
+        nc.vector.tensor_copy(plane(0, b0, nb), window(0, b0, nb))
+        for t in range(PACK - 1):
+            gather_bare(t, a0, na)
+        cuts_a = ((a0, BANK), (a0 + BANK, BANK))
+        for s, m in cuts_a:
+            gather_bare(PACK - 1, s, m)
+        for t in range(PACK):
+            gather_gated(t, 0, OWN)
+        for s, m in ((0, OWN // 2), (OWN // 2, OWN // 2)):
+            weave(s, m)
+        for i, (s, m) in enumerate(cuts_a):
+            gate_and_weave(s, m, gate_in_psum(s, m, 6 + i))
+        for t in range(1, PACK):
+            gather_bare(t, b0, nb)
+        for t in range(PACK):
+            gather_bare(t, c0, nc_)
+        quantize(0, 1024)
+        gate_and_weave(b0, nb, gate_sb[:, b0:c0])
+        quantize(1024, 512)
+        quantize(1536, 256)
+        gate_and_weave(c0, nc_, gate_sb[:, c0:S])
+        quantize(b0, nb)
+        quantize(c0, nc_)
+
+        dx = [placed.tile([P, S], F32, name="dx%d" % j, offset=4 * S * (j + 1)) for j in range(KT - 1)]
+        for j, s, m, bank in ((0, 0, 512, 0), (0, 512, 512, 1), (1, 0, 512, 6), (1, 512, 512, 7), (0, 1024, 512, 2), (0, 1536, 256, 3), (1, 1024, 512, 0)):
+            empty(*multiply(j, s, m, bank))
+        last = [multiply(0, b0, nb, 4)]
+        empty(*multiply(1, 1536, BANK, 1))
+        last.append(multiply(0, c0, nc_, 5))
+        for sums in last:
+            empty_on_vector(*sums)
+        empty_on_vector(*multiply(1, 2048, BANK, 4))
 
         def listed(j, r, t0, t1):
             return dx[j][:].indirect(pos_sb[r][:, t0 // 16 : t1 // 16])
@@ -200,25 +215,45 @@ def tile_moe_bdx_lin_none_kernel(tc, dyT, w_words, w_scales, gate, offs, pos1, p
         head0 = placed.tile([P, T], F32, name="head0", offset=0)
         shared = keep.tile([P, 2 * T - TOKEN_CUT], F32, name="shared")
         sum0 = fetch_bare(0, 0, head0[:], halves)
-        heads1 = [fetch_bare(1, r, fresh("head1_%d" % r), whole) for r in range(2)]
+        head1 = fetch_bare(1, 0, fresh("head1"), whole)
         sum0 = fetch(0, 1, shared[:, T - TOKEN_CUT :], sum0, halves)
         dx.append(placed.tile([P, S], F32, name="dx2", offset=0))
-        for i, bank in enumerate((6, 7, 0, 4, 1)):
+        for i, bank in enumerate((6, 7, 0, 1, 5)):
             empty(*multiply(2, BANK * i, BANK, bank))
-        heads2 = [fetch_bare(2, r, fresh("head2_%d" % r), LAST_CUTS if r == 2 else whole) for r in range(TOP - 1)]
+        parts = [fetch_bare(2, r, fresh("part%d" % r), whole) for r in range(2)]
+        parts.append(fetch_bare(2, 2, fresh("part2"), ((HELPED, LAST_CUTS[0][1]), LAST_CUTS[1])))
+        parts.append(fresh("part3"))
         sum0 = fetch(0, 2, fresh("sum0_2"), sum0, halves)
-        low1 = fetch(1, 2, shared[:, 0:T], heads1[0], whole)
+        sum1 = fetch(1, 1, shared[:, 0:T], head1, whole)
         sum0 = fetch(0, 3, fresh("sum0_3"), sum0, whole)
         nc.sync.dma_start(out[0:P, :], sum0)
-        high1 = fetch(1, 3, fresh("high1"), heads1[1], whole)
-        sum2 = fetch(2, 3, fresh("sum2_3"), heads2[0], whole)
-        sum1 = fresh("sum1")
-        nc.vector.tensor_tensor(sum1, low1, high1, ADD)
-        nc.sync.dma_start(out[P : 2 * P, :], sum1)
-        more2 = fresh("more2")
-        for t0, t1 in LAST_CUTS:
-            nc.vector.tensor_tensor(more2[:, t0:t1], sum2[:, t0:t1], heads2[1][:, t0:t1], ADD)
-        total = fresh("total")
-        for t0, t1 in LAST_CUTS:
-            nc.vector.tensor_tensor(total[:, t0:t1], more2[:, t0:t1], heads2[2][:, t0:t1], ADD)
-            nc.sync.dma_start(out[2 * P :, t0:t1], total[:, t0:t1])
+        nc.vector.tensor_copy(parts[3], listed(2, 3, 0, T))
+        nc.vector.tensor_copy(parts[2][:, 0:HELPED], listed(2, 2, 0, HELPED))
+        turned = [psum.tile([P, BANK], F32, name="bank%d" % bank) for bank in (2, 3)]
+        order = (0, 3, 1, 2)
+        for r in order:
+            for acc, (t0, t1) in zip(turned, LAST_CUTS):
+                for t in range(t0, t1, P):
+                    nc.tensor.matmul(
+                        acc[:, t - t0 : t - t0 + P],
+                        parts[r][:, t : t + P],
+                        ident[:],
+                        is_transpose=True,
+                        start=(r == order[0] and t == t0),
+                        stop=(r == order[-1] and t + P == t1),
+                    )
+        sum1 = fetch(1, 2, parts[0], sum1, LAST_CUTS)
+        total1 = fresh("total1")
+        for cut in LAST_CUTS:
+            fetch(1, 3, total1, sum1, (cut,))
+            nc.sync.dma_start(out[P : 2 * P, cut[0] : cut[1]], total1[:, cut[0] : cut[1]])
+        by_token = fresh("by_token")
+        total2 = fresh("total2")
+        for acc, (t0, t1) in zip(turned, LAST_CUTS):
+            nc.scalar.copy(by_token[:, t0:t1], acc[:, 0 : t1 - t0])
+        for bank, (t0, t1) in zip((5, 6), LAST_CUTS):
+            acc = psum.tile([P, BANK], F32, name="bank%d" % bank)
+            for t in range(t0, t1, P):
+                nc.tensor.transpose(acc[:, t - t0 : t - t0 + P], by_token[:, t : t + P], ident[:])
+            nc.scalar.copy(total2[:, t0:t1], acc[:, 0 : t1 - t0])
+            nc.sync.dma_start(out[2 * P :, t0:t1], total2[:, t0:t1])

from contextlib import ExitStack

import concourse.mybir as mybir
from concourse.masks import make_identity

K, T, E, C, N = 384, 640, 20, 128, 512
TOP = 4
S = E * C

FLOPS = 2 * K * N * S
BYTES = 4 * N * T + E * 128 * 768 + E * 16 * K + 4 * S + 2 * 128 * (S // 16) * 2 + 4 * K * T

F32 = mybir.dt.float32
BF16 = mybir.dt.bfloat16
I32 = mybir.dt.int32
U32 = mybir.dt.uint32
U16 = mybir.dt.uint16
U8 = mybir.dt.uint8
FP8X4 = mybir.dt.float8_e4m3fn_x4
FP4X4 = mybir.dt.float4_e2m1fn_x4
MULT = mybir.AluOpType.mult
ADD = mybir.AluOpType.add
COPY = mybir.ActivationFunctionType.Copy

P = 128
PACK = 4
KT = K // P
BANK = 512
OWN = 768
CHUNKS = (1024, 512, 256)
TOKEN_CUT = 256
LAST_CUTS = ((0, 384), (384, 640))
HELPED = 256


def starts(widths, first=0):
    return [first + sum(widths[:i]) for i in range(len(widths))]


def tile_moe_bdx_lin_none_kernel(tc, dyT, w_words, w_scales, gate, offs, pos1, pos2, pos3, pos4, out):
    nc = tc.nc
    with ExitStack() as ctx:
        lists = ctx.enter_context(tc.tile_pool(name="lists", bufs=1))
        keep = ctx.enter_context(tc.tile_pool(name="keep", bufs=1))
        placed = ctx.enter_context(tc.tile_pool(name="placed", bufs=1))
        psum = ctx.enter_context(tc.psum_pool(name="psum", bufs=1))

        a0, b0, c0 = starts(CHUNKS, OWN)
        offs_sb = lists.tile([P, S // 16], U16, name="offs_sb")
        pos_sb = [lists.tile([P, T // 16], U16, name="pos_sb%d" % r) for r in range(TOP)]
        dy = [keep.tile([P, max(CHUNKS) + 16], F32, name="dy%d" % t) for t in range(PACK - 1)]
        dy.append(placed.tile([P, max(CHUNKS) + 16], F32, name="dy3", offset=8 * S - 2048))
        w_sb = keep.tile([P, E, 2 * K], U8, name="w_sb", align_bytes=64)
        ws_sb = keep.tile([P, E, K], U8, name="ws_sb", align_bytes=64)
        gate_sb = keep.tile([P, S], F32, name="gate_sb")
        na, nb, nc_ = CHUNKS
        pitch_b = PACK * na + nc_
        at_a = 2 * pitch_b
        planes = keep.tile([P, PACK * pitch_b], F32, name="planes")
        planes_own = keep.tile([P, PACK * OWN], F32, name="planes_own")
        gate_own = planes[:, pitch_b : pitch_b + OWN]
        regions = (
            (0, planes_own[:]),
            (a0, planes[:, at_a : at_a + PACK * na]),
            (b0, planes[:]),
            (c0, planes[:, at_a + na : at_a + (PACK + 1) * na]),
        )
        grouped = keep.tile([P, S, PACK], BF16, name="grouped", align_bytes=64)
        g_codes = keep.tile([P, S], U32, name="g_codes", align_bytes=64)
        g_scales = keep.tile([P, S], U8, name="g_scales", align_bytes=64)

        nc.vector.memset(ws_sb[:, 0:2].bitcast(I32), 0)
        nc.scalar.copy(ws_sb[:, 2:4].bitcast(U32), ws_sb[:, 0:2].bitcast(U32))
        nc.vector.memset(ws_sb[:, 4:].bitcast(I32), 0)
        ident = keep.tile([P, P], F32, name="ident")
        make_identity(nc, ident[:])

        dy_rows = dyT.rearrange("(p t) j -> p t j", t=PACK)
        nc.sync.dma_start(offs_sb[:], offs)
        for t in range(PACK):
            nc.sync.dma_start(dy[t][:, 0:T], dy_rows[:, t, :])
            if t == 0:
                nc.sync.dma_start(gate_own, gate[0:P, 0:a0])
        gate_col = keep.tile([P, na // C], F32, name="gate_col")
        with nc.allow_non_contiguous_dma(reason="one gate a partition"):
            nc.sync.dma_start(gate_col[:], gate[0, a0:b0].rearrange("(e c) -> c e", c=C))
        nc.sync.dma_start(gate_sb[:, b0:S], gate[0:P, b0:S])
        by_partition = w_words[:, 0].rearrange("e p b -> p e b")
        for e0 in (0, E // 2):
            nc.sync.dma_start(w_sb[:, e0 : e0 + E // 2].bitcast(I32), by_partition[:, e0 : e0 + E // 2].bitcast(I32))
        for r, pos in enumerate((pos1, pos2, pos3, pos4)):
            nc.sync.dma_start(pos_sb[r][:], pos)
        for r in range(4):
            nc.sync.dma_start(
                ws_sb[r:P:32].bitcast(I32),
                w_scales[:, 0, r:16:4, :].rearrange("e q k -> q e k").bitcast(I32),
            )

        def region(s, m):
            s0, rows = [r for r in regions if r[0] <= s][-1]
            return rows.rearrange("p (t s) -> p t s", t=PACK)[:, :, s - s0 : s - s0 + m]

        def plane(t, s, m):
            return region(s, m)[:, t, :]

        def window(t, s, m):
            return dy[t][:].indirect(offs_sb[:, s // 16 : (s + m) // 16])

        def gather_bare(t, s, m):
            nc.scalar.activation(plane(t, s, m), window(t, s, m), COPY)

        def gather_gated(t, s, m):
            nc.vector.tensor_tensor(plane(t, s, m), window(t, s, m), gate_own[:, s : s + m], MULT)

        def woven(s, m):
            return grouped[:, s : s + m, :].rearrange("p (a i) t -> p a t i", i=4)

        def four_planes(s, m):
            return region(s, m).rearrange("p t (a i) -> p a t i", i=4)

        def weave(s, m):
            nc.gpsimd.tensor_scalar(woven(s, m), four_planes(s, m), 1.0, 0.0, MULT, ADD)

        def gate_and_weave(s, m, gates):
            spread = gates.rearrange("p (a i) -> p a i", i=4).unsqueeze(2).to_broadcast([P, m // 4, PACK, 4])
            nc.vector.tensor_tensor(woven(s, m), four_planes(s, m), spread, MULT)

        def quantize(s, m):
            nc.vector.quantize_mx(
                out=g_codes[:, s : s + m].bitcast(FP8X4),
                scales=g_scales[:, s : s + m],
                in_=grouped[:, s : s + m, :].rearrange("p s t -> p (s t)"),
            )

        def multiply(j, s0, n, bank):
            acc = psum.tile([P, BANK], F32, name="bank%d" % bank)
            for s in range(s0, s0 + n, C):
                e = s // C
                nc.tensor.matmul_mx(
                    out=acc[:, s - s0 : s - s0 + C],
                    lhsT=w_sb[:, e, 2 * P * j : 2 * P * (j + 1)].bitcast(FP4X4),
                    lhsT_scale=ws_sb[:, e, P * j : P * (j + 1)],
                    rhs=g_codes[:, s : s + C].bitcast(FP8X4),
                    rhs_scale=g_scales[:, s : s + C],
                    start=True,
                    stop=True,
                )
            return j, s0, n, acc

        def empty(j, s0, n, acc):
            nc.scalar.copy(dx[j][:, s0 : s0 + n], acc[:, 0:n])

        def empty_on_vector(j, s0, n, acc):
            nc.vector.tensor_copy(dx[j][:, s0 : s0 + n], acc[:, 0:n])

        def gate_in_psum(s, m, bank):
            acc = psum.tile([P, BANK], F32, name="bank%d" % bank)
            for i in range(m // C):
                e = (s - a0) // C + i
                nc.tensor.transpose(acc[:, C * i : C * (i + 1)], gate_col[:, e : e + 1].to_broadcast([P, P]), ident[:])
            return acc[:, 0:m]

        nc.vector.tensor_copy(plane(0, b0, nb), window(0, b0, nb))
        for t in range(PACK - 1):
            gather_bare(t, a0, na)
        cuts_a = ((a0, BANK), (a0 + BANK, BANK))
        for s, m in cuts_a:
            gather_bare(PACK - 1, s, m)
        for t in range(PACK):
            gather_gated(t, 0, OWN)
        for s, m in ((0, OWN // 2), (OWN // 2, OWN // 2)):
            weave(s, m)
        for i, (s, m) in enumerate(cuts_a):
            gate_and_weave(s, m, gate_in_psum(s, m, 6 + i))
        for t in range(1, PACK):
            gather_bare(t, b0, nb)
        for t in range(PACK):
            gather_bare(t, c0, nc_)
        quantize(0, 1024)
        gate_and_weave(b0, nb, gate_sb[:, b0:c0])
        quantize(1024, 512)
        quantize(1536, 256)
        gate_and_weave(c0, nc_, gate_sb[:, c0:S])
        quantize(b0, nb)
        quantize(c0, nc_)

        dx = [placed.tile([P, S], F32, name="dx%d" % j, offset=4 * S * (j + 1)) for j in range(KT - 1)]
        for j, s, m, bank in ((0, 0, 512, 0), (0, 512, 512, 1), (1, 0, 512, 6), (1, 512, 512, 7), (0, 1024, 512, 2), (0, 1536, 256, 3), (1, 1024, 512, 0)):
            empty(*multiply(j, s, m, bank))
        last = [multiply(0, b0, nb, 4)]
        empty(*multiply(1, 1536, BANK, 1))
        last.append(multiply(0, c0, nc_, 5))
        for sums in last:
            empty_on_vector(*sums)
        empty_on_vector(*multiply(1, 2048, BANK, 4))

        def listed(j, r, t0, t1):
            return dx[j][:].indirect(pos_sb[r][:, t0 // 16 : t1 // 16])

        def fetch_bare(j, r, got, cuts):
            for t0, t1 in cuts:
                nc.scalar.activation(got[:, t0:t1], listed(j, r, t0, t1), COPY)
            return got

        def fetch(j, r, total, partial, cuts):
            for t0, t1 in cuts:
                nc.vector.tensor_tensor(total[:, t0:t1], listed(j, r, t0, t1), partial[:, t0:t1], ADD)
            return total

        def fresh(name):
            return keep.tile([P, T], F32, name=name)[:]

        halves = ((0, TOKEN_CUT), (TOKEN_CUT, T))
        whole = ((0, T),)
        head0 = placed.tile([P, T], F32, name="head0", offset=0)
        shared = keep.tile([P, 2 * T - TOKEN_CUT], F32, name="shared")
        sum0 = fetch_bare(0, 0, head0[:], halves)
        head1 = fetch_bare(1, 0, fresh("head1"), whole)
        sum0 = fetch(0, 1, shared[:, T - TOKEN_CUT :], sum0, halves)
        dx.append(placed.tile([P, S], F32, name="dx2", offset=0))
        for i, bank in enumerate((6, 7, 0, 1, 5)):
            empty(*multiply(2, BANK * i, BANK, bank))
        parts = [fetch_bare(2, r, fresh("part%d" % r), whole) for r in range(2)]
        parts.append(fetch_bare(2, 2, fresh("part2"), ((HELPED, LAST_CUTS[0][1]), LAST_CUTS[1])))
        parts.append(fresh("part3"))
        sum0 = fetch(0, 2, fresh("sum0_2"), sum0, halves)
        sum1 = fetch(1, 1, shared[:, 0:T], head1, whole)
        sum0 = fetch(0, 3, fresh("sum0_3"), sum0, whole)
        nc.sync.dma_start(out[0:P, :], sum0)
        nc.vector.tensor_copy(parts[3], listed(2, 3, 0, T))
        nc.vector.tensor_copy(parts[2][:, 0:HELPED], listed(2, 2, 0, HELPED))
        turned = [psum.tile([P, BANK], F32, name="bank%d" % bank) for bank in (2, 3)]
        order = (0, 3, 1, 2)
        for r in order:
            for acc, (t0, t1) in zip(turned, LAST_CUTS):
                for t in range(t0, t1, P):
                    nc.tensor.matmul(
                        acc[:, t - t0 : t - t0 + P],
                        parts[r][:, t : t + P],
                        ident[:],
                        is_transpose=True,
                        start=(r == order[0] and t == t0),
                        stop=(r == order[-1] and t + P == t1),
                    )
        sum1 = fetch(1, 2, parts[0], sum1, LAST_CUTS)
        total1 = fresh("total1")
        for cut in LAST_CUTS:
            fetch(1, 3, total1, sum1, (cut,))
            nc.sync.dma_start(out[P : 2 * P, cut[0] : cut[1]], total1[:, cut[0] : cut[1]])
        by_token = fresh("by_token")
        total2 = fresh("total2")
        for acc, (t0, t1) in zip(turned, LAST_CUTS):
            nc.scalar.copy(by_token[:, t0:t1], acc[:, 0 : t1 - t0])
        for bank, (t0, t1) in zip((5, 6), LAST_CUTS):
            acc = psum.tile([P, BANK], F32, name="bank%d" % bank)
            for t in range(t0, t1, P):
                nc.tensor.transpose(acc[:, t - t0 : t - t0 + P], by_token[:, t : t + P], ident[:])
            nc.scalar.copy(total2[:, t0:t1], acc[:, 0 : t1 - t0])
            nc.sync.dma_start(out[2 * P :, t0:t1], total2[:, t0:t1])
